import numpy as np
import ml_dtypes


def mxq(x, axis, fmt="e4m3"):
    dtype, down = {"e4m3": (ml_dtypes.float8_e4m3fn, 7), "e5m2": (ml_dtypes.float8_e5m2, 14)}[fmt]
    v = np.moveaxis(np.asarray(x, np.float32).astype(ml_dtypes.bfloat16).astype(np.float64), axis, -1)
    blocks = v.reshape(v.shape[:-1] + (-1, 32))
    amax = np.abs(blocks).max(-1, keepdims=True)
    byte = np.maximum(np.where(amax > 0, np.frexp(amax)[1] - 1 + 127, 0) - down, 1)
    scale = np.exp2(byte - 127.0)
    codes = (blocks / scale).astype(np.float32).astype(dtype).astype(np.float64)
    return np.moveaxis((codes * scale).reshape(v.shape), -1, axis)


WIDE = False


def mx_kscale(k):
    if not WIDE:
        return np.ones(k)
    levels = np.array([10, -10, 5, -5, 0])
    if k % 512:
        return np.exp2(np.random.permutation(np.resize(levels, k // 32))).repeat(32)
    a = np.empty((k // 512, 16))
    for p in range(k // 512):
        a[p, :8] = np.random.permutation(np.resize(levels, 8))
        for g in range(8):
            far = levels[np.abs(levels - a[p, g]) >= 10]
            a[p, g + 8] = far[np.random.randint(len(far))]
    return np.exp2(a.ravel()).repeat(32)


def f64(x):
    return np.asarray(x).astype(np.float64)


def striped(idx):
    return np.tile(idx.reshape(-1, 16).T, (8, 1)).astype(np.uint16)


def unstriped(offs):
    return offs[:16].T.reshape(-1).astype(np.int64)


E2M1 = np.array([0.0, 0.5, 1.0, 1.5, 2.0, 3.0, 4.0, 6.0, -0.0, -0.5, -1.0, -1.5, -2.0, -3.0, -4.0, -6.0])


def pack_weight(w, fmt):
    k, n = w.shape
    w = f64(np.asarray(w, np.float32).astype(ml_dtypes.bfloat16)).reshape(k // 32, 32, n)
    amax = np.abs(w).max(1)
    if fmt == "e4m3":
        byte = np.frexp(amax)[1] - 1 + 127 - 7
    else:
        mant, ex = np.frexp(amax / 6.0)
        byte = np.where(mant > 0.5, ex, ex - 1) + 127
    byte = np.clip(np.where(amax > 0, byte, 1), 1, 254)
    scaled = (w * np.exp2(127.0 - byte)[:, None, :]).reshape(k, n).astype(np.float32)
    by_word = np.ascontiguousarray(scaled.reshape(k // 512, 128, 4, n).transpose(0, 1, 3, 2))
    if fmt == "e4m3":
        words = by_word.astype(ml_dtypes.float8_e4m3fn).view(np.uint8)
    else:
        c = by_word.astype(ml_dtypes.float4_e2m1fn).view(np.uint8) & 0xF
        words = (c[..., 0::2] | (c[..., 1::2] << 4)).reshape(k // 512, 128, 2 * n)
    return np.ascontiguousarray(words), np.ascontiguousarray(byte.astype(np.uint8).reshape(k // 512, 16, n))


def unpack_weight(words, scales, fmt):
    g, _, n = scales.shape
    words = np.ascontiguousarray(words).reshape(g, 128, n, -1)
    if fmt == "e4m3":
        vals = words.view(ml_dtypes.float8_e4m3fn).astype(np.float64)
    else:
        nib = np.empty((g, 128, n, 4), np.uint8)
        nib[..., 0::2] = words & 0xF
        nib[..., 1::2] = words >> 4
        vals = E2M1[nib]
    vals = vals * np.repeat(np.exp2(scales.astype(np.float64) - 127.0), 8, axis=1)[..., None]
    return vals.transpose(0, 1, 3, 2).reshape(g * 512, n)


K, T, E, C, N = 1024, 512, 6, 128, 256


def by_expert(wq, xq):
    return np.concatenate([wq[e].T @ xq[:, e * C:(e + 1) * C] for e in range(E)], axis=1)


def setup_inputs():
    n = np.random.standard_normal
    s = mx_kscale(K)
    slot_token = np.concatenate([np.random.permutation(T)[:C] for e in range(E)])
    x = pack_weight(n((K, T)) * s[:, None], "e4m3")
    wq = [pack_weight(m, "e2m1") for m in n((E, K, N)) / np.sqrt(K) / s[None, :, None]]
    wk = [pack_weight(m, "e4m3") for m in n((E, K, N)) / np.sqrt(K) / s[None, :, None]]
    return {
        "x_words": x[0],
        "x_scales": x[1],
        "wq_words": np.stack([m[0] for m in wq]),
        "wq_scales": np.stack([m[1] for m in wq]),
        "wk_words": np.stack([m[0] for m in wk]),
        "wk_scales": np.stack([m[1] for m in wk]),
        "wv": (n((E, K, N)) / np.sqrt(K) / s[None, :, None]).astype(np.float32),
        "bias": (0.3 * n((3 * N, E))).astype(np.float32),
        "offs": striped(slot_token),
    }


def reference(x_words, x_scales, wq_words, wq_scales, wk_words, wk_scales, wv, bias, offs):
    wq = np.stack([unpack_weight(wq_words[e], wq_scales[e], "e2m1") for e in range(E)])
    wk = np.stack([unpack_weight(wk_words[e], wk_scales[e], "e4m3") for e in range(E)])
    wvq = mxq(f64(wv), 1, "e4m3")
    idx = unstriped(offs)
    xq = unpack_weight(x_words, x_scales, "e4m3")[:, idx]
    y = np.concatenate([by_expert(w, xq) for w in (wq, wk, wvq)])
    y = y + np.repeat(f64(bias), C, axis=1)
    out = y
    return out

@@ -1,0 +1,197 @@
+from contextlib import ExitStack
+
+import concourse.mybir as mybir
+
+K, T, E, C, N = 1024, 512, 6, 128, 256
+FLOPS = 2 * K * 3 * N * E * C
+
+F32 = mybir.dt.float32
+BF16 = mybir.dt.bfloat16
+I32 = mybir.dt.int32
+U32 = mybir.dt.uint32
+U16 = mybir.dt.uint16
+U8 = mybir.dt.uint8
+FP8X4 = mybir.dt.float8_e4m3fn_x4
+FP4X4 = mybir.dt.float4_e2m1fn_x4
+IDENTITY = mybir.ActivationFunctionType.Identity
+
+P = 128
+PACK = 4
+PASSES = K // (P * PACK)
+HALVES = N // P
+SLOTS = E * C
+GROUP = 3
+GROUP_SLOTS = GROUP * C
+WK_ROW = 4
+BIAS_PAD = 8
+EARLY_V = 4
+
+
+def tile_moe_qkv_s_kernel(
+    tc, x_words, x_scales, wq_words, wq_scales, wk_words, wk_scales, wv, bias, offs, out
+):
+    nc = tc.nc
+    with ExitStack() as ctx:
+        held = ctx.enter_context(tc.tile_pool(name="held", bufs=1))
+        psum = ctx.enter_context(tc.psum_pool(name="psum", bufs=8))
+
+        offsets = held.tile([P, SLOTS // 16], U16, name="offsets")
+        tok_words = held.tile([P, PASSES * T], I32, name="tok_words", align_bytes=64)
+        tok_scales = held.tile([P, PASSES * T], U8, name="tok_scales", align_bytes=64)
+        q_codes = held.tile([P, E * PASSES, 2 * N], U8, name="q_codes", align_bytes=64)
+        k_codes = held.tile([P, E * PASSES, N], I32, name="k_codes", align_bytes=64)
+        qk_scales = held.tile([P, E * PASSES * N], U8, name="qk_scales", align_bytes=64)
+        bias_sb = held.tile([P, 3 * HALVES, BIAS_PAD], F32, name="bias_sb")
+        v_raw = [
+            [held.tile([P, PACK, N], F32, name=f"v_raw{e}_{s}") for s in range(PASSES)]
+            if e == E - 1 else None
+            for e in range(E)
+        ]
+        v_whole = [held.tile([P, PASSES, PACK, N], F32, name=f"v_whole{e}") for e in range(E - 1)]
+        for e in range(E - 1):
+            v_raw[e] = [v_whole[e][:, s] for s in range(PASSES)]
+        v_raw[E - 1] = [t[:] for t in v_raw[E - 1]]
+
+        nc.vector.memset(tok_scales[:].bitcast(I32), 0)
+        nc.vector.memset(qk_scales[:].bitcast(I32), 0)
+
+        def load_scale_rows(plane, first_row, src):
+            groups = src.shape[0]
+            by_row = src.rearrange("g (q r) n -> r q g n", r=4)
+            words = plane[:].bitcast(I32).rearrange("p (g w) -> p g w", g=groups)
+            for r in range(4):
+                nc.sync.dma_start(out=words[first_row + r : P : 32], in_=by_row[r].bitcast(I32))
+
+        def load_v(e):
+            nc.sync.dma_start(
+                out=v_whole[e][:].rearrange("p s j n -> p s (j n)"),
+                in_=wv[e].rearrange("(s p j) n -> p s (j n)", s=PASSES, j=PACK),
+            )
+
+        nc.sync.dma_start(offsets[:], offs)
+        nc.sync.dma_start(
+            out=tok_words[:].rearrange("p (s t) -> p s t", s=PASSES),
+            in_=x_words.rearrange("s p t d -> p s (t d)").bitcast(I32),
+        )
+        load_scale_rows(tok_scales, 0, x_scales)
+        load_v(0)
+        load_scale_rows(qk_scales, 0, wq_scales.rearrange("e s b n -> (e s) b n"))
+        nc.sync.dma_start(
+            out=q_codes[:].bitcast(I32),
+            in_=wq_words.rearrange("e s p b -> p (e s) b").bitcast(I32),
+        )
+        load_scale_rows(qk_scales, WK_ROW, wk_scales.rearrange("e s b n -> (e s) b n"))
+        nc.sync.dma_start(
+            out=k_codes[:],
+            in_=wk_words.rearrange("e s p n d -> p (e s) (n d)").bitcast(I32),
+        )
+        nc.sync.dma_start(out=bias_sb[:, :, 0:E], in_=bias.rearrange("(t p) e -> p t e", p=P))
+        for e in range(1, E - 1):
+            load_v(e)
+        for s in range(PASSES):
+            nc.sync.dma_start(
+                out=v_raw[E - 1][s].rearrange("p j n -> p (j n)"),
+                in_=wv[E - 1, s * P * PACK : (s + 1) * P * PACK].rearrange("(p j) n -> p (j n)", j=PACK),
+            )
+
+        slot_words, slot_scales = {}, {}
+        for g in range(E // GROUP):
+            listed = offsets[:, g * GROUP_SLOTS // 16 : (g + 1) * GROUP_SLOTS // 16]
+            for s in range(PASSES):
+                slot_words[g, s] = held.tile([P, GROUP_SLOTS], U32, name=f"slot_words{g}_{s}", align_bytes=64)
+                window = tok_words[:, s * T : (s + 1) * T].bitcast(U32)
+                nc.vector.tensor_copy(slot_words[g, s][:], window.indirect(listed))
+            for s in range(PASSES):
+                slot_scales[g, s] = held.tile([P, GROUP_SLOTS], U8, name=f"slot_scales{g}_{s}", align_bytes=64)
+                window = tok_scales[:, s * T : (s + 1) * T]
+                nc.vector.tensor_copy(slot_scales[g, s][:], window.indirect(listed))
+
+        def project(e, proj, codes, scales, result):
+            g, u = divmod(e, GROUP)
+            cols = slice(u * C, (u + 1) * C)
+            acc = psum.tile([P, HALVES, C], F32, name="acc")
+            for h in range(HALVES):
+                for s in range(PASSES):
+                    nc.tensor.matmul_mx(
+                        out=acc[:, h, :],
+                        lhsT=codes(s, h),
+                        lhsT_scale=scales(s, h),
+                        rhs=slot_words[g, s][:, cols].bitcast(FP8X4),
+                        rhs_scale=slot_scales[g, s][:, cols],
+                        start=(s == 0),
+                        stop=(s == PASSES - 1),
+                    )
+            for h in range(HALVES):
+                nc.scalar.activation(
+                    out=result[:, h, :], in_=acc[:, h, :], func=IDENTITY,
+                    bias=bias_sb[:, proj * HALVES + h, e : e + 1],
+                )
+
+        def store(proj, first, staged):
+            width = staged.shape[2]
+            rows = out[proj * N : (proj + 1) * N, first : first + width]
+            nc.sync.dma_start(out=rows.rearrange("(h p) j -> p h j", p=P), in_=staged[:])
+
+        v_codes, v_scales = {}, {}
+
+        def quantize_v(e):
+            grouped = []
+            for s in range(PASSES):
+                tile = held.tile([P, N, PACK], BF16, name=f"v_grouped{e}_{s}", align_bytes=64)
+                src = v_raw[e][s].rearrange("p j n -> p n j")
+                if s == 0:
+                    nc.scalar.copy(out=tile[:], in_=src)
+                else:
+                    nc.vector.tensor_copy(out=tile[:], in_=src)
+                grouped.append(tile)
+            for s in range(PASSES):
+                v_codes[e, s] = held.tile([P, N], U32, name=f"v_codes{e}_{s}", align_bytes=64)
+                v_scales[e, s] = held.tile([P, N], U8, name=f"v_scales{e}_{s}", align_bytes=64)
+                nc.vector.quantize_mx(
+                    out=v_codes[e, s][:].bitcast(FP8X4),
+                    scales=v_scales[e, s][:],
+                    in_=grouped[s][:].rearrange("p n j -> p (n j)"),
+                )
+
+        def plane_cols(e, s, h):
+            first = (e * PASSES + s) * N + h * P
+            return slice(first, first + P)
+
+        q_out = held.tile([P, HALVES, SLOTS], F32, name="q_out")
+        k_out = held.tile([P, HALVES, SLOTS], F32, name="k_out")
+        v_early = held.tile([P, HALVES, EARLY_V * C], F32, name="v_early")
+        v_late = held.tile([P, HALVES, (E - EARLY_V) * C], F32, name="v_late")
+
+        quantize_v(0)
+        for e in range(E):
+            project(
+                e, 0,
+                lambda s, h, e=e: q_codes[:, e * PASSES + s, h * 2 * P : (h + 1) * 2 * P].bitcast(FP4X4),
+                lambda s, h, e=e: qk_scales[:, plane_cols(e, s, h)],
+                q_out[:, :, e * C : (e + 1) * C],
+            )
+        store(0, 0, q_out)
+        for e in range(E):
+            project(
+                e, 1,
+                lambda s, h, e=e: k_codes[:, e * PASSES + s, h * P : (h + 1) * P].bitcast(FP8X4),
+                lambda s, h, e=e: qk_scales[WK_ROW:P, plane_cols(e, s, h)],
+                k_out[:, :, e * C : (e + 1) * C],
+            )
+        store(1, 0, k_out)
+        for e in range(E):
+            if e > 0:
+                quantize_v(e)
+            if e < EARLY_V:
+                result = v_early[:, :, e * C : (e + 1) * C]
+            else:
+                result = v_late[:, :, (e - EARLY_V) * C : (e - EARLY_V + 1) * C]
+            project(
+                e, 2,
+                lambda s, h, e=e: v_codes[e, s][:, h * P : (h + 1) * P].bitcast(FP8X4),
+                lambda s, h, e=e: v_scales[e, s][:, h * P : (h + 1) * P],
+                result,
+            )
+            if e == EARLY_V - 1:
+                store(2, 0, v_early)
+        store(2, EARLY_V * C, v_late)

@@ -1,6 +1,7 @@
 from contextlib import ExitStack
 
 import concourse.mybir as mybir
+from concourse.masks import make_identity
 
 K, T, E, C, N = 1024, 512, 6, 128, 256
 FLOPS = 2 * K * 3 * N * E * C
@@ -13,6 +14,7 @@ U16 = mybir.dt.uint16
 U8 = mybir.dt.uint8
 FP8X4 = mybir.dt.float8_e4m3fn_x4
 FP4X4 = mybir.dt.float4_e2m1fn_x4
+ADD = mybir.AluOpType.add
 IDENTITY = mybir.ActivationFunctionType.Identity
 
 P = 128
@@ -23,8 +25,10 @@ SLOTS = E * C
 GROUP = 3
 GROUP_SLOTS = GROUP * C
 WK_ROW = 4
-BIAS_PAD = 8
-EARLY_V = 4
+TILES = 3 * HALVES
+PER_BANK = 4
+SCALAR_ONLY_V = 2
+EARLY_V = E - 1
 
 
 def tile_moe_qkv_s_kernel(
@@ -33,15 +37,19 @@ def tile_moe_qkv_s_kernel(
     nc = tc.nc
     with ExitStack() as ctx:
         held = ctx.enter_context(tc.tile_pool(name="held", bufs=1))
-        psum = ctx.enter_context(tc.psum_pool(name="psum", bufs=8))
+        psum = ctx.enter_context(tc.psum_pool(name="psum", bufs=6))
+        psum_bias = ctx.enter_context(tc.psum_pool(name="psum_bias", bufs=1))
 
         offsets = held.tile([P, SLOTS // 16], U16, name="offsets")
         tok_words = held.tile([P, PASSES * T], I32, name="tok_words", align_bytes=64)
         tok_scales = held.tile([P, PASSES * T], U8, name="tok_scales", align_bytes=64)
         q_codes = held.tile([P, E * PASSES, 2 * N], U8, name="q_codes", align_bytes=64)
         k_codes = held.tile([P, E * PASSES, N], I32, name="k_codes", align_bytes=64)
-        qk_scales = held.tile([P, E * PASSES * N], U8, name="qk_scales", align_bytes=64)
-        bias_sb = held.tile([P, 3 * HALVES, BIAS_PAD], F32, name="bias_sb")
+        q_scales = held.tile([P, E * PASSES * N], U8, name="q_scales", align_bytes=64)
+        k_scales = held.tile([P, E * PASSES * N], U8, name="k_scales", align_bytes=64)
+        bias_rows = held.tile([P, P * E], F32, name="bias_rows")
+        bias_sb = held.tile([P, E, TILES], F32, name="bias_sb")
+        identity = held.tile([P, P], F32, name="identity")
         v_raw = [
             [held.tile([P, PACK, N], F32, name=f"v_raw{e}_{s}") for s in range(PASSES)]
             if e == E - 1 else None
@@ -53,7 +61,9 @@ def tile_moe_qkv_s_kernel(
         v_raw[E - 1] = [t[:] for t in v_raw[E - 1]]
 
         nc.vector.memset(tok_scales[:].bitcast(I32), 0)
-        nc.vector.memset(qk_scales[:].bitcast(I32), 0)
+        nc.vector.memset(k_scales[:].bitcast(I32), 0)
+        nc.vector.memset(bias_rows[:], 0.0)
+        nc.vector.memset(q_scales[:].bitcast(I32), 0)
 
         def load_scale_rows(plane, first_row, src):
             groups = src.shape[0]
@@ -73,21 +83,23 @@ def tile_moe_qkv_s_kernel(
             out=tok_words[:].rearrange("p (s t) -> p s t", s=PASSES),
             in_=x_words.rearrange("s p t d -> p s (t d)").bitcast(I32),
         )
-        load_scale_rows(tok_scales, 0, x_scales)
         load_v(0)
-        load_scale_rows(qk_scales, 0, wq_scales.rearrange("e s b n -> (e s) b n"))
-        nc.sync.dma_start(
-            out=q_codes[:].bitcast(I32),
-            in_=wq_words.rearrange("e s p b -> p (e s) b").bitcast(I32),
-        )
-        load_scale_rows(qk_scales, WK_ROW, wk_scales.rearrange("e s b n -> (e s) b n"))
+        load_scale_rows(tok_scales, 0, x_scales)
+        load_v(1)
         nc.sync.dma_start(
             out=k_codes[:],
             in_=wk_words.rearrange("e s p n d -> p (e s) (n d)").bitcast(I32),
         )
-        nc.sync.dma_start(out=bias_sb[:, :, 0:E], in_=bias.rearrange("(t p) e -> p t e", p=P))
-        for e in range(1, E - 1):
-            load_v(e)
+        load_scale_rows(k_scales, WK_ROW, wk_scales.rearrange("e s b n -> (e s) b n"))
+        nc.sync.dma_start(out=bias_rows[0:TILES, :], in_=bias.rearrange("(t p) e -> t (p e)", p=P))
+        load_v(2)
+        nc.sync.dma_start(
+            out=q_codes[:].bitcast(I32),
+            in_=wq_words.rearrange("e s p b -> p (e s) b").bitcast(I32),
+        )
+        load_scale_rows(q_scales, 0, wq_scales.rearrange("e s b n -> (e s) b n"))
+        load_v(3)
+        load_v(4)
         for s in range(PASSES):
             nc.sync.dma_start(
                 out=v_raw[E - 1][s].rearrange("p j n -> p (j n)"),
@@ -101,10 +113,21 @@ def tile_moe_qkv_s_kernel(
                 slot_words[g, s] = held.tile([P, GROUP_SLOTS], U32, name=f"slot_words{g}_{s}", align_bytes=64)
                 window = tok_words[:, s * T : (s + 1) * T].bitcast(U32)
                 nc.vector.tensor_copy(slot_words[g, s][:], window.indirect(listed))
+        for g in range(E // GROUP):
+            listed = offsets[:, g * GROUP_SLOTS // 16 : (g + 1) * GROUP_SLOTS // 16]
             for s in range(PASSES):
                 slot_scales[g, s] = held.tile([P, GROUP_SLOTS], U8, name=f"slot_scales{g}_{s}", align_bytes=64)
                 window = tok_scales[:, s * T : (s + 1) * T]
                 nc.vector.tensor_copy(slot_scales[g, s][:], window.indirect(listed))
+
+        make_identity(nc, identity[:])
+        by_expert = bias_rows[:].rearrange("t (p e) -> t e p", e=E)
+        for first in range(0, E, PER_BANK):
+            count = min(PER_BANK, E - first)
+            turned = psum_bias.tile([P, count, P], F32, name=f"turned{first}")
+            for i in range(count):
+                nc.tensor.transpose(turned[:, i, :], by_expert[:, first + i, :], identity[:])
+            nc.scalar.copy(out=bias_sb[:, first : first + count, :], in_=turned[:, :, 0:TILES])
 
         def project(e, proj, codes, scales, result):
             g, u = divmod(e, GROUP)
@@ -121,11 +144,15 @@ def tile_moe_qkv_s_kernel(
                         start=(s == 0),
                         stop=(s == PASSES - 1),
                     )
-            for h in range(HALVES):
-                nc.scalar.activation(
-                    out=result[:, h, :], in_=acc[:, h, :], func=IDENTITY,
-                    bias=bias_sb[:, proj * HALVES + h, e : e + 1],
-                )
+            columns = bias_sb[:, e, proj * HALVES : (proj + 1) * HALVES]
+            if proj == 1:
+                spread = columns.unsqueeze(2).to_broadcast([P, HALVES, C])
+                nc.vector.tensor_tensor(out=result, in0=acc[:], in1=spread, op=ADD)
+            else:
+                for h in range(HALVES):
+                    nc.scalar.activation(
+                        out=result[:, h, :], in_=acc[:, h, :], func=IDENTITY, bias=columns[:, h : h + 1]
+                    )
 
         def store(proj, first, staged):
             width = staged.shape[2]
@@ -138,11 +165,12 @@ def tile_moe_qkv_s_kernel(
             grouped = []
             for s in range(PASSES):
                 tile = held.tile([P, N, PACK], BF16, name=f"v_grouped{e}_{s}", align_bytes=64)
-                src = v_raw[e][s].rearrange("p j n -> p n j")
-                if s == 0:
-                    nc.scalar.copy(out=tile[:], in_=src)
+                src = v_raw[e][s].rearrange("p j (c i) -> p c j i", i=4)
+                dst = tile[:].rearrange("p (c i) j -> p c j i", i=4)
+                if s == 0 or e < SCALAR_ONLY_V:
+                    nc.scalar.copy(out=dst, in_=src)
                 else:
-                    nc.vector.tensor_copy(out=tile[:], in_=src)
+                    nc.vector.tensor_copy(out=dst, in_=src)
                 grouped.append(tile)
             for s in range(PASSES):
                 v_codes[e, s] = held.tile([P, N], U32, name=f"v_codes{e}_{s}", align_bytes=64)
@@ -162,36 +190,75 @@ def tile_moe_qkv_s_kernel(
         v_early = held.tile([P, HALVES, EARLY_V * C], F32, name="v_early")
         v_late = held.tile([P, HALVES, (E - EARLY_V) * C], F32, name="v_late")
 
-        quantize_v(0)
-        for e in range(E):
+        def project_v(e):
             project(
-                e, 0,
-                lambda s, h, e=e: q_codes[:, e * PASSES + s, h * 2 * P : (h + 1) * 2 * P].bitcast(FP4X4),
-                lambda s, h, e=e: qk_scales[:, plane_cols(e, s, h)],
-                q_out[:, :, e * C : (e + 1) * C],
+                e, 2,
+                lambda s, h: v_codes[e, s][:, h * P : (h + 1) * P].bitcast(FP8X4),
+                lambda s, h: v_scales[e, s][:, h * P : (h + 1) * P],
+                v_early[:, :, e * C : (e + 1) * C],
             )
-        store(0, 0, q_out)
+
+        for e in range(SCALAR_ONLY_V):
+            quantize_v(e)
         for e in range(E):
             project(
                 e, 1,
                 lambda s, h, e=e: k_codes[:, e * PASSES + s, h * P : (h + 1) * P].bitcast(FP8X4),
-                lambda s, h, e=e: qk_scales[WK_ROW:P, plane_cols(e, s, h)],
+                lambda s, h, e=e: k_scales[WK_ROW:P, plane_cols(e, s, h)],
                 k_out[:, :, e * C : (e + 1) * C],
             )
         store(1, 0, k_out)
+        for e in range(SCALAR_ONLY_V):
+            project_v(e)
+        quantize_v(2)
+        project_v(2)
         for e in range(E):
-            if e > 0:
-                quantize_v(e)
-            if e < EARLY_V:
-                result = v_early[:, :, e * C : (e + 1) * C]
-            else:
-                result = v_late[:, :, (e - EARLY_V) * C : (e - EARLY_V + 1) * C]
             project(
-                e, 2,
-                lambda s, h, e=e: v_codes[e, s][:, h * P : (h + 1) * P].bitcast(FP8X4),
-                lambda s, h, e=e: v_scales[e, s][:, h * P : (h + 1) * P],
-                result,
+                e, 0,
+                lambda s, h, e=e: q_codes[:, e * PASSES + s, h * 2 * P : (h + 1) * 2 * P].bitcast(FP4X4),
+                lambda s, h, e=e: q_scales[:, plane_cols(e, s, h)],
+                q_out[:, :, e * C : (e + 1) * C],
             )
-            if e == EARLY_V - 1:
-                store(2, 0, v_early)
+        store(0, 0, q_out)
+        for e in range(3, EARLY_V):
+            quantize_v(e)
+            project_v(e)
+        store(2, 0, v_early)
+
+        e = E - 1
+        g, u = divmod(e, GROUP)
+        cols = slice(u * C, (u + 1) * C)
+        accs = [psum.tile([P, C], F32, name="acc") for h in range(HALVES)]
+        for s in range(PASSES):
+            pieces = []
+            for h in range(HALVES):
+                tile = held.tile([P, P, PACK], BF16, name=f"last_grouped{s}_{h}", align_bytes=64)
+                src = v_raw[e][s][:, :, h * P : (h + 1) * P].rearrange("p j (c i) -> p c j i", i=4)
+                dst = tile[:].rearrange("p (c i) j -> p c j i", i=4)
+                if h == 0:
+                    nc.vector.tensor_copy(out=dst, in_=src)
+                else:
+                    nc.scalar.copy(out=dst, in_=src)
+                pieces.append(tile)
+            for h in range(HALVES):
+                codes = held.tile([P, P], U32, name=f"last_codes{s}_{h}", align_bytes=64)
+                scales = held.tile([P, P], U8, name=f"last_scales{s}_{h}", align_bytes=64)
+                nc.vector.quantize_mx(
+                    out=codes[:].bitcast(FP8X4), scales=scales[:],
+                    in_=pieces[h][:].rearrange("p n j -> p (n j)"),
+                )
+                nc.tensor.matmul_mx(
+                    out=accs[h][:],
+                    lhsT=codes[:].bitcast(FP8X4),
+                    lhsT_scale=scales[:],
+                    rhs=slot_words[g, s][:, cols].bitcast(FP8X4),
+                    rhs_scale=slot_scales[g, s][:, cols],
+                    start=(s == 0),
+                    stop=(s == PASSES - 1),
+                )
+        columns = bias_sb[:, e, 2 * HALVES : 3 * HALVES]
+        nc.vector.tensor_scalar(
+            out=v_late[:, 0, :], in0=accs[0][:], scalar1=columns[:, 0:1], scalar2=None, op0=ADD
+        )
+        nc.scalar.activation(out=v_late[:, 1, :], in_=accs[1][:], func=IDENTITY, bias=columns[:, 1:2])
         store(2, EARLY_V * C, v_late)

@@ -27,7 +27,8 @@ GROUP_SLOTS = GROUP * C
 WK_ROW = 4
 TILES = 3 * HALVES
 PER_BANK = 4
-SCALAR_ONLY_V = 2
+SCALAR_V = 4
+RING = 4
 EARLY_V = E - 1
 
 
@@ -37,46 +38,40 @@ def tile_moe_qkv_s_kernel(
     nc = tc.nc
     with ExitStack() as ctx:
         held = ctx.enter_context(tc.tile_pool(name="held", bufs=1))
+        stream = ctx.enter_context(tc.tile_pool(name="stream", bufs=RING))
         psum = ctx.enter_context(tc.psum_pool(name="psum", bufs=6))
         psum_bias = ctx.enter_context(tc.psum_pool(name="psum_bias", bufs=1))
 
         offsets = held.tile([P, SLOTS // 16], U16, name="offsets")
         tok_words = held.tile([P, PASSES * T], I32, name="tok_words", align_bytes=64)
         tok_scales = held.tile([P, PASSES * T], U8, name="tok_scales", align_bytes=64)
-        q_codes = held.tile([P, E * PASSES, 2 * N], U8, name="q_codes", align_bytes=64)
-        k_codes = held.tile([P, E * PASSES, N], I32, name="k_codes", align_bytes=64)
         q_scales = held.tile([P, E * PASSES * N], U8, name="q_scales", align_bytes=64)
         k_scales = held.tile([P, E * PASSES * N], U8, name="k_scales", align_bytes=64)
         bias_rows = held.tile([P, P * E], F32, name="bias_rows")
         bias_sb = held.tile([P, E, TILES], F32, name="bias_sb")
         identity = held.tile([P, P], F32, name="identity")
-        v_raw = [
-            [held.tile([P, PACK, N], F32, name=f"v_raw{e}_{s}") for s in range(PASSES)]
-            if e == E - 1 else None
-            for e in range(E)
-        ]
-        v_whole = [held.tile([P, PASSES, PACK, N], F32, name=f"v_whole{e}") for e in range(E - 1)]
-        for e in range(E - 1):
-            v_raw[e] = [v_whole[e][:, s] for s in range(PASSES)]
-        v_raw[E - 1] = [t[:] for t in v_raw[E - 1]]
+        v_raw = {}
 
+        nc.gpsimd.memset(bias_rows[:], 0.0)
         nc.vector.memset(tok_scales[:].bitcast(I32), 0)
         nc.vector.memset(k_scales[:].bitcast(I32), 0)
-        nc.vector.memset(bias_rows[:], 0.0)
         nc.vector.memset(q_scales[:].bitcast(I32), 0)
 
-        def load_scale_rows(plane, first_row, src):
+        def load_scale_rows(queue, plane, first_row, src):
             groups = src.shape[0]
             by_row = src.rearrange("g (q r) n -> r q g n", r=4)
             words = plane[:].bitcast(I32).rearrange("p (g w) -> p g w", g=groups)
             for r in range(4):
-                nc.sync.dma_start(out=words[first_row + r : P : 32], in_=by_row[r].bitcast(I32))
+                queue.dma_start(out=words[first_row + r : P : 32], in_=by_row[r].bitcast(I32))
 
-        def load_v(e):
-            nc.sync.dma_start(
-                out=v_whole[e][:].rearrange("p s j n -> p s (j n)"),
-                in_=wv[e].rearrange("(s p j) n -> p s (j n)", s=PASSES, j=PACK),
-            )
+        def load_v(e, pieces=1):
+            raw = stream.tile([P, PASSES, PACK, N], F32, name="v_raw", tag="weights", align_bytes=64)
+            dst = raw[:].rearrange("p s j n -> p s (j n)")
+            src = wv[e].rearrange("(s p j) n -> p s (j n)", s=PASSES, j=PACK)
+            step = PASSES // pieces
+            for s in range(0, PASSES, step):
+                nc.sync.dma_start(out=dst[:, s : s + step], in_=src[:, s : s + step])
+            v_raw[e] = [raw[:, s] for s in range(PASSES)]
 
         nc.sync.dma_start(offsets[:], offs)
         nc.sync.dma_start(
@@ -84,27 +79,12 @@ def tile_moe_qkv_s_kernel(
             in_=x_words.rearrange("s p t d -> p s (t d)").bitcast(I32),
         )
         load_v(0)
-        load_scale_rows(tok_scales, 0, x_scales)
-        load_v(1)
-        nc.sync.dma_start(
-            out=k_codes[:],
-            in_=wk_words.rearrange("e s p n d -> p (e s) (n d)").bitcast(I32),
-        )
-        load_scale_rows(k_scales, WK_ROW, wk_scales.rearrange("e s b n -> (e s) b n"))
+        load_scale_rows(nc.sync, tok_scales, 0, x_scales)
         nc.sync.dma_start(out=bias_rows[0:TILES, :], in_=bias.rearrange("(t p) e -> t (p e)", p=P))
-        load_v(2)
-        nc.sync.dma_start(
-            out=q_codes[:].bitcast(I32),
-            in_=wq_words.rearrange("e s p b -> p (e s) b").bitcast(I32),
-        )
-        load_scale_rows(q_scales, 0, wq_scales.rearrange("e s b n -> (e s) b n"))
-        load_v(3)
-        load_v(4)
-        for s in range(PASSES):
-            nc.sync.dma_start(
-                out=v_raw[E - 1][s].rearrange("p j n -> p (j n)"),
-                in_=wv[E - 1, s * P * PACK : (s + 1) * P * PACK].rearrange("(p j) n -> p (j n)", j=PACK),
-            )
+        load_scale_rows(nc.gpsimd, k_scales, WK_ROW, wk_scales.rearrange("e s b n -> (e s) b n"))
+        load_scale_rows(nc.gpsimd, q_scales, 0, wq_scales.rearrange("e s b n -> (e s) b n"))
+        for e in range(1, SCALAR_V):
+            load_v(e)
 
         slot_words, slot_scales = {}, {}
         for g in range(E // GROUP):
@@ -120,32 +100,37 @@ def tile_moe_qkv_s_kernel(
                 window = tok_scales[:, s * T : (s + 1) * T]
                 nc.vector.tensor_copy(slot_scales[g, s][:], window.indirect(listed))
 
-        make_identity(nc, identity[:])
-        by_expert = bias_rows[:].rearrange("t (p e) -> t e p", e=E)
-        for first in range(0, E, PER_BANK):
-            count = min(PER_BANK, E - first)
-            turned = psum_bias.tile([P, count, P], F32, name=f"turned{first}")
-            for i in range(count):
-                nc.tensor.transpose(turned[:, i, :], by_expert[:, first + i, :], identity[:])
-            nc.scalar.copy(out=bias_sb[:, first : first + count, :], in_=turned[:, :, 0:TILES])
+        def turn_bias():
+            make_identity(nc, identity[:])
+            by_expert = bias_rows[:].rearrange("t (p e) -> t e p", e=E)
+            for first in range(0, E, PER_BANK):
+                count = min(PER_BANK, E - first)
+                turned = psum_bias.tile([P, count, P], F32, name=f"turned{first}")
+                for i in range(count):
+                    nc.tensor.transpose(turned[:, i, :], by_expert[:, first + i, :], identity[:])
+                nc.vector.tensor_copy(out=bias_sb[:, first : first + count, :], in_=turned[:, :, 0:TILES])
 
-        def project(e, proj, codes, scales, result):
+        def multiply(acc, e, s, codes, scales):
             g, u = divmod(e, GROUP)
             cols = slice(u * C, (u + 1) * C)
+            nc.tensor.matmul_mx(
+                out=acc,
+                lhsT=codes,
+                lhsT_scale=scales,
+                rhs=slot_words[g, s][:, cols].bitcast(FP8X4),
+                rhs_scale=slot_scales[g, s][:, cols],
+                start=(s == 0),
+                stop=(s == PASSES - 1),
+            )
+
+        def project(e, proj, codes, scales, staged, on_vector):
+            result = staged[:, :, e * C : (e + 1) * C]
             acc = psum.tile([P, HALVES, C], F32, name="acc")
             for h in range(HALVES):
                 for s in range(PASSES):
-                    nc.tensor.matmul_mx(
-                        out=acc[:, h, :],
-                        lhsT=codes(s, h),
-                        lhsT_scale=scales(s, h),
-                        rhs=slot_words[g, s][:, cols].bitcast(FP8X4),
-                        rhs_scale=slot_scales[g, s][:, cols],
-                        start=(s == 0),
-                        stop=(s == PASSES - 1),
-                    )
+                    multiply(acc[:, h, :], e, s, codes(s, h), scales(s, h))
             columns = bias_sb[:, e, proj * HALVES : (proj + 1) * HALVES]
-            if proj == 1:
+            if on_vector:
                 spread = columns.unsqueeze(2).to_broadcast([P, HALVES, C])
                 nc.vector.tensor_tensor(out=result, in0=acc[:], in1=spread, op=ADD)
             else:
@@ -159,27 +144,36 @@ def tile_moe_qkv_s_kernel(
             rows = out[proj * N : (proj + 1) * N, first : first + width]
             nc.sync.dma_start(out=rows.rearrange("(h p) j -> p h j", p=P), in_=staged[:])
 
-        v_codes, v_scales = {}, {}
+        v_grouped, v_codes, v_scales = {}, {}, {}
+
+        def round_piece(key, raw, on_vector):
+            width = raw.shape[2]
+            tile = held.tile([P, width, PACK], BF16, name="v_grouped%d_%d_%d" % key, align_bytes=64)
+            src = raw.rearrange("p j (c i) -> p c j i", i=4)
+            dst = tile[:].rearrange("p (c i) j -> p c j i", i=4)
+            if on_vector:
+                nc.vector.tensor_copy(out=dst, in_=src)
+            else:
+                nc.scalar.copy(out=dst, in_=src)
+            v_grouped[key] = tile
+
+        def quantize_piece(key):
+            width = v_grouped[key].shape[1]
+            v_codes[key] = held.tile([P, width], U32, name="v_codes%d_%d_%d" % key, align_bytes=64)
+            v_scales[key] = held.tile([P, width], U8, name="v_scales%d_%d_%d" % key, align_bytes=64)
+            nc.vector.quantize_mx(
+                out=v_codes[key][:].bitcast(FP8X4),
+                scales=v_scales[key][:],
+                in_=v_grouped[key][:].rearrange("p n j -> p (n j)"),
+            )
+
+        def round_v(e):
+            for s in range(PASSES):
+                round_piece((e, s, 0), v_raw[e][s], on_vector=(e >= SCALAR_V))
 
         def quantize_v(e):
-            grouped = []
             for s in range(PASSES):
-                tile = held.tile([P, N, PACK], BF16, name=f"v_grouped{e}_{s}", align_bytes=64)
-                src = v_raw[e][s].rearrange("p j (c i) -> p c j i", i=4)
-                dst = tile[:].rearrange("p (c i) j -> p c j i", i=4)
-                if s == 0 or e < SCALAR_ONLY_V:
-                    nc.scalar.copy(out=dst, in_=src)
-                else:
-                    nc.vector.tensor_copy(out=dst, in_=src)
-                grouped.append(tile)
-            for s in range(PASSES):
-                v_codes[e, s] = held.tile([P, N], U32, name=f"v_codes{e}_{s}", align_bytes=64)
-                v_scales[e, s] = held.tile([P, N], U8, name=f"v_scales{e}_{s}", align_bytes=64)
-                nc.vector.quantize_mx(
-                    out=v_codes[e, s][:].bitcast(FP8X4),
-                    scales=v_scales[e, s][:],
-                    in_=grouped[s][:].rearrange("p n j -> p (n j)"),
-                )
+                quantize_piece((e, s, 0))
 
         def plane_cols(e, s, h):
             first = (e * PASSES + s) * N + h * P
@@ -188,75 +182,81 @@ def tile_moe_qkv_s_kernel(
         q_out = held.tile([P, HALVES, SLOTS], F32, name="q_out")
         k_out = held.tile([P, HALVES, SLOTS], F32, name="k_out")
         v_early = held.tile([P, HALVES, EARLY_V * C], F32, name="v_early")
-        v_late = held.tile([P, HALVES, (E - EARLY_V) * C], F32, name="v_late")
+        v_late = held.tile([P, HALVES, C], F32, name="v_late")
+
+        def project_q(e):
+            project(
+                e, 0,
+                lambda s, h: q_codes[:, e * PASSES + s, h * 2 * P : (h + 1) * 2 * P].bitcast(FP4X4),
+                lambda s, h: q_scales[:, plane_cols(e, s, h)],
+                q_out, on_vector=(e % 2 == 0),
+            )
+
+        def project_k(e):
+            project(
+                e, 1,
+                lambda s, h: k_codes[:, e * PASSES + s, h * P : (h + 1) * P].bitcast(FP8X4),
+                lambda s, h: k_scales[WK_ROW:P, plane_cols(e, s, h)],
+                k_out, on_vector=False,
+            )
 
         def project_v(e):
             project(
                 e, 2,
-                lambda s, h: v_codes[e, s][:, h * P : (h + 1) * P].bitcast(FP8X4),
-                lambda s, h: v_scales[e, s][:, h * P : (h + 1) * P],
-                v_early[:, :, e * C : (e + 1) * C],
+                lambda s, h: v_codes[e, s, 0][:, h * P : (h + 1) * P].bitcast(FP8X4),
+                lambda s, h: v_scales[e, s, 0][:, h * P : (h + 1) * P],
+                v_early, on_vector=True,
             )
 
-        for e in range(SCALAR_ONLY_V):
+        last = E - 1
+
+        round_v(0)
+        k_codes = stream.tile([P, E * PASSES, N], I32, name="k_codes", tag="weights", align_bytes=64)
+        nc.sync.dma_start(
+            out=k_codes[:],
+            in_=wk_words.rearrange("e s p n d -> p (e s) (n d)").bitcast(I32),
+        )
+        round_v(1)
+        load_v(4)
+        round_v(2)
+        q_codes = stream.tile([P, E * PASSES, 2 * N], U8, name="q_codes", tag="weights", align_bytes=64)
+        nc.sync.dma_start(
+            out=q_codes[:].bitcast(I32),
+            in_=wq_words.rearrange("e s p b -> p (e s) b").bitcast(I32),
+        )
+        round_v(3)
+        load_v(last, pieces=PASSES)
+        turn_bias()
+        for e in range(SCALAR_V):
             quantize_v(e)
+            if e > 0:
+                project_v(e - 1)
+        round_v(4)
+        project_v(3)
         for e in range(E):
-            project(
-                e, 1,
-                lambda s, h, e=e: k_codes[:, e * PASSES + s, h * P : (h + 1) * P].bitcast(FP8X4),
-                lambda s, h, e=e: k_scales[WK_ROW:P, plane_cols(e, s, h)],
-                k_out[:, :, e * C : (e + 1) * C],
-            )
+            project_k(e)
         store(1, 0, k_out)
-        for e in range(SCALAR_ONLY_V):
-            project_v(e)
-        quantize_v(2)
-        project_v(2)
-        for e in range(E):
-            project(
-                e, 0,
-                lambda s, h, e=e: q_codes[:, e * PASSES + s, h * 2 * P : (h + 1) * 2 * P].bitcast(FP4X4),
-                lambda s, h, e=e: q_scales[:, plane_cols(e, s, h)],
-                q_out[:, :, e * C : (e + 1) * C],
-            )
-        store(0, 0, q_out)
-        for e in range(3, EARLY_V):
-            quantize_v(e)
-            project_v(e)
+        quantize_v(4)
+        project_v(4)
         store(2, 0, v_early)
-
-        e = E - 1
-        g, u = divmod(e, GROUP)
-        cols = slice(u * C, (u + 1) * C)
+        for e in range(3):
+            project_q(e)
+        round_piece((last, 0, 0), v_raw[last][0], on_vector=True)
+        project_q(3)
+        quantize_piece((last, 0, 0))
+        project_q(4)
+        project_q(5)
+        store(0, 0, q_out)
         accs = [psum.tile([P, C], F32, name="acc") for h in range(HALVES)]
-        for s in range(PASSES):
-            pieces = []
-            for h in range(HALVES):
-                tile = held.tile([P, P, PACK], BF16, name=f"last_grouped{s}_{h}", align_bytes=64)
-                src = v_raw[e][s][:, :, h * P : (h + 1) * P].rearrange("p j (c i) -> p c j i", i=4)
-                dst = tile[:].rearrange("p (c i) j -> p c j i", i=4)
-                if h == 0:
-                    nc.vector.tensor_copy(out=dst, in_=src)
-                else:
-                    nc.scalar.copy(out=dst, in_=src)
-                pieces.append(tile)
-            for h in range(HALVES):
-                codes = held.tile([P, P], U32, name=f"last_codes{s}_{h}", align_bytes=64)
-                scales = held.tile([P, P], U8, name=f"last_scales{s}_{h}", align_bytes=64)
-                nc.vector.quantize_mx(
-                    out=codes[:].bitcast(FP8X4), scales=scales[:],
-                    in_=pieces[h][:].rearrange("p n j -> p (n j)"),
-                )
-                nc.tensor.matmul_mx(
-                    out=accs[h][:],
-                    lhsT=codes[:].bitcast(FP8X4),
-                    lhsT_scale=scales[:],
-                    rhs=slot_words[g, s][:, cols].bitcast(FP8X4),
-                    rhs_scale=slot_scales[g, s][:, cols],
-                    start=(s == 0),
-                    stop=(s == PASSES - 1),
-                )
-        columns = bias_sb[:, e, 2 * HALVES : 3 * HALVES]
+        for h in range(HALVES):
+            cols = slice(h * P, (h + 1) * P)
+            multiply(accs[h][:], last, 0, v_codes[last, 0, 0][:, cols].bitcast(FP8X4), v_scales[last, 0, 0][:, cols])
+        for h in range(HALVES):
+            round_piece((last, 1, h), v_raw[last][1][:, :, h * P : (h + 1) * P], on_vector=(h == 0))
+        for h in range(HALVES):
+            quantize_piece((last, 1, h))
+            multiply(accs[h][:], last, 1, v_codes[last, 1, h][:].bitcast(FP8X4), v_scales[last, 1, h][:])
+        columns = bias_sb[:, last, 2 * HALVES : 3 * HALVES]
         nc.vector.tensor_scalar(
             out=v_late[:, 0, :], in0=accs[0][:], scalar1=columns[:, 0:1], scalar2=None, op0=ADD
         )

@@ -29,6 +29,7 @@ TILES = 3 * HALVES
 PER_BANK = 4
 SCALAR_V = 4
 RING = 4
+BIAS_ROW = 16
 EARLY_V = E - 1
 
 
@@ -80,7 +81,7 @@ def tile_moe_qkv_s_kernel(
         )
         load_v(0)
         load_scale_rows(nc.sync, tok_scales, 0, x_scales)
-        nc.sync.dma_start(out=bias_rows[0:TILES, :], in_=bias.rearrange("(t p) e -> t (p e)", p=P))
+        nc.sync.dma_start(out=bias_rows[BIAS_ROW : BIAS_ROW + TILES, :], in_=bias.rearrange("(t p) e -> t (p e)", p=P))
         load_scale_rows(nc.gpsimd, k_scales, WK_ROW, wk_scales.rearrange("e s b n -> (e s) b n"))
         load_scale_rows(nc.gpsimd, q_scales, 0, wq_scales.rearrange("e s b n -> (e s) b n"))
         for e in range(1, SCALAR_V):
@@ -108,7 +109,7 @@ def tile_moe_qkv_s_kernel(
                 turned = psum_bias.tile([P, count, P], F32, name=f"turned{first}")
                 for i in range(count):
                     nc.tensor.transpose(turned[:, i, :], by_expert[:, first + i, :], identity[:])
-                nc.vector.tensor_copy(out=bias_sb[:, first : first + count, :], in_=turned[:, :, 0:TILES])
+                nc.vector.tensor_copy(out=bias_sb[:, first : first + count, :], in_=turned[:, :, BIAS_ROW : BIAS_ROW + TILES])
 
         def multiply(acc, e, s, codes, scales):
             g, u = divmod(e, GROUP)
@@ -220,10 +221,10 @@ def tile_moe_qkv_s_kernel(
         load_v(4)
         round_v(2)
         q_codes = stream.tile([P, E * PASSES, 2 * N], U8, name="q_codes", tag="weights", align_bytes=64)
-        nc.sync.dma_start(
-            out=q_codes[:].bitcast(I32),
-            in_=wq_words.rearrange("e s p b -> p (e s) b").bitcast(I32),
-        )
+        q_source = wq_words.rearrange("e s p b -> p (e s) b").bitcast(I32)
+        for g in range(E // GROUP):
+            part = slice(g * GROUP * PASSES, (g + 1) * GROUP * PASSES)
+            nc.sync.dma_start(out=q_codes[:].bitcast(I32)[:, part, :], in_=q_source[:, part, :])
         round_v(3)
         load_v(last, pieces=PASSES)
         turn_bias()

@@ -18,6 +18,7 @@ ADD = mybir.AluOpType.add
 IDENTITY = mybir.ActivationFunctionType.Identity
 
 P = 128
+ALIGN = 256
 PACK = 4
 PASSES = K // (P * PACK)
 HALVES = N // P
@@ -43,12 +44,12 @@ def tile_moe_qkv_s_kernel(
         psum = ctx.enter_context(tc.psum_pool(name="psum", bufs=6))
         psum_bias = ctx.enter_context(tc.psum_pool(name="psum_bias", bufs=1))
 
-        offsets = held.tile([P, SLOTS // 16], U16, name="offsets")
-        tok_words = held.tile([P, PASSES * T], I32, name="tok_words", align_bytes=64)
-        tok_scales = held.tile([P, PASSES * T], U8, name="tok_scales", align_bytes=64)
-        q_scales = held.tile([P, E * PASSES * N], U8, name="q_scales", align_bytes=64)
-        k_scales = held.tile([P, E * PASSES * N], U8, name="k_scales", align_bytes=64)
-        bias_rows = held.tile([P, P * E], F32, name="bias_rows")
+        offsets = held.tile([P, SLOTS // 16], U16, name="offsets", align_bytes=ALIGN)
+        tok_words = held.tile([P, PASSES * T], I32, name="tok_words", align_bytes=ALIGN)
+        tok_scales = held.tile([P, PASSES * T], U8, name="tok_scales", align_bytes=ALIGN)
+        q_scales = held.tile([P, E * PASSES * N], U8, name="q_scales", align_bytes=ALIGN)
+        k_scales = held.tile([P, E * PASSES * N], U8, name="k_scales", align_bytes=ALIGN)
+        bias_rows = held.tile([P, P * E], F32, name="bias_rows", align_bytes=ALIGN)
         bias_sb = held.tile([P, E, TILES], F32, name="bias_sb")
         identity = held.tile([P, P], F32, name="identity")
         v_raw = {}
@@ -66,7 +67,7 @@ def tile_moe_qkv_s_kernel(
                 queue.dma_start(out=words[first_row + r : P : 32], in_=by_row[r].bitcast(I32))
 
         def load_v(e, pieces=1):
-            raw = stream.tile([P, PASSES, PACK, N], F32, name="v_raw", tag="weights", align_bytes=64)
+            raw = stream.tile([P, PASSES, PACK, N], F32, name="v_raw", tag="weights", align_bytes=ALIGN)
             dst = raw[:].rearrange("p s j n -> p s (j n)")
             src = wv[e].rearrange("(s p j) n -> p s (j n)", s=PASSES, j=PACK)
             step = PASSES // pieces
@@ -91,13 +92,13 @@ def tile_moe_qkv_s_kernel(
         for g in range(E // GROUP):
             listed = offsets[:, g * GROUP_SLOTS // 16 : (g + 1) * GROUP_SLOTS // 16]
             for s in range(PASSES):
-                slot_words[g, s] = held.tile([P, GROUP_SLOTS], U32, name=f"slot_words{g}_{s}", align_bytes=64)
+                slot_words[g, s] = held.tile([P, GROUP_SLOTS], U32, name=f"slot_words{g}_{s}", align_bytes=ALIGN)
                 window = tok_words[:, s * T : (s + 1) * T].bitcast(U32)
                 nc.vector.tensor_copy(slot_words[g, s][:], window.indirect(listed))
         for g in range(E // GROUP):
             listed = offsets[:, g * GROUP_SLOTS // 16 : (g + 1) * GROUP_SLOTS // 16]
             for s in range(PASSES):
-                slot_scales[g, s] = held.tile([P, GROUP_SLOTS], U8, name=f"slot_scales{g}_{s}", align_bytes=64)
+                slot_scales[g, s] = held.tile([P, GROUP_SLOTS], U8, name=f"slot_scales{g}_{s}", align_bytes=ALIGN)
                 window = tok_scales[:, s * T : (s + 1) * T]
                 nc.vector.tensor_copy(slot_scales[g, s][:], window.indirect(listed))
 
@@ -149,7 +150,7 @@ def tile_moe_qkv_s_kernel(
 
         def round_piece(key, raw, on_vector):
             width = raw.shape[2]
-            tile = held.tile([P, width, PACK], BF16, name="v_grouped%d_%d_%d" % key, align_bytes=64)
+            tile = held.tile([P, width, PACK], BF16, name="v_grouped%d_%d_%d" % key, align_bytes=ALIGN)
             src = raw.rearrange("p j (c i) -> p c j i", i=4)
             dst = tile[:].rearrange("p (c i) j -> p c j i", i=4)
             if on_vector:
@@ -160,8 +161,8 @@ def tile_moe_qkv_s_kernel(
 
         def quantize_piece(key):
             width = v_grouped[key].shape[1]
-            v_codes[key] = held.tile([P, width], U32, name="v_codes%d_%d_%d" % key, align_bytes=64)
-            v_scales[key] = held.tile([P, width], U8, name="v_scales%d_%d_%d" % key, align_bytes=64)
+            v_codes[key] = held.tile([P, width], U32, name="v_codes%d_%d_%d" % key, align_bytes=ALIGN)
+            v_scales[key] = held.tile([P, width], U8, name="v_scales%d_%d_%d" % key, align_bytes=ALIGN)
             nc.vector.quantize_mx(
                 out=v_codes[key][:].bitcast(FP8X4),
                 scales=v_scales[key][:],
@@ -180,10 +181,10 @@ def tile_moe_qkv_s_kernel(
             first = (e * PASSES + s) * N + h * P
             return slice(first, first + P)
 
-        q_out = held.tile([P, HALVES, SLOTS], F32, name="q_out")
-        k_out = held.tile([P, HALVES, SLOTS], F32, name="k_out")
-        v_early = held.tile([P, HALVES, EARLY_V * C], F32, name="v_early")
-        v_late = held.tile([P, HALVES, C], F32, name="v_late")
+        q_out = held.tile([P, HALVES, SLOTS], F32, name="q_out", align_bytes=ALIGN)
+        k_out = held.tile([P, HALVES, SLOTS], F32, name="k_out", align_bytes=ALIGN)
+        v_early = held.tile([P, HALVES, EARLY_V * C], F32, name="v_early", align_bytes=ALIGN)
+        v_late = held.tile([P, HALVES, C], F32, name="v_late", align_bytes=ALIGN)
 
         def project_q(e):
             project(
@@ -212,7 +213,7 @@ def tile_moe_qkv_s_kernel(
         last = E - 1
 
         round_v(0)
-        k_codes = stream.tile([P, E * PASSES, N], I32, name="k_codes", tag="weights", align_bytes=64)
+        k_codes = stream.tile([P, E * PASSES, N], I32, name="k_codes", tag="weights", align_bytes=ALIGN)
         nc.sync.dma_start(
             out=k_codes[:],
             in_=wk_words.rearrange("e s p n d -> p (e s) (n d)").bitcast(I32),
@@ -220,7 +221,7 @@ def tile_moe_qkv_s_kernel(
         round_v(1)
         load_v(4)
         round_v(2)
-        q_codes = stream.tile([P, E * PASSES, 2 * N], U8, name="q_codes", tag="weights", align_bytes=64)
+        q_codes = stream.tile([P, E * PASSES, 2 * N], U8, name="q_codes", tag="weights", align_bytes=ALIGN)
         q_source = wq_words.rearrange("e s p b -> p (e s) b").bitcast(I32)
         for g in range(E // GROUP):
             part = slice(g * GROUP * PASSES, (g + 1) * GROUP * PASSES)

@@ -19,12 +19,12 @@ IDENTITY = mybir.ActivationFunctionType.Identity
 
 P = 128
 ALIGN = 256
+PAGE = 4096
 PACK = 4
 PASSES = K // (P * PACK)
 HALVES = N // P
 SLOTS = E * C
 GROUP = 3
-GROUP_SLOTS = GROUP * C
 WK_ROW = 4
 TILES = 3 * HALVES
 PER_BANK = 4
@@ -45,8 +45,8 @@ def tile_moe_qkv_s_kernel(
         psum_bias = ctx.enter_context(tc.psum_pool(name="psum_bias", bufs=1))
 
         offsets = held.tile([P, SLOTS // 16], U16, name="offsets", align_bytes=ALIGN)
-        tok_words = held.tile([P, PASSES * T], I32, name="tok_words", align_bytes=ALIGN)
-        tok_scales = held.tile([P, PASSES * T], U8, name="tok_scales", align_bytes=ALIGN)
+        tok_words = held.tile([P, (PASSES + 1) * T], I32, name="tok_words", align_bytes=PAGE)
+        tok_scales = held.tile([P, (PASSES + 1) * T], U8, name="tok_scales", align_bytes=ALIGN)
         q_scales = held.tile([P, E * PASSES * N], U8, name="q_scales", align_bytes=ALIGN)
         k_scales = held.tile([P, E * PASSES * N], U8, name="k_scales", align_bytes=ALIGN)
         bias_rows = held.tile([P, P * E], F32, name="bias_rows", align_bytes=ALIGN)
@@ -58,16 +58,17 @@ def tile_moe_qkv_s_kernel(
         nc.vector.memset(tok_scales[:].bitcast(I32), 0)
         nc.vector.memset(k_scales[:].bitcast(I32), 0)
         nc.vector.memset(q_scales[:].bitcast(I32), 0)
+        nc.vector.memset(tok_words[:, PASSES * T :], 0)
 
         def load_scale_rows(queue, plane, first_row, src):
             groups = src.shape[0]
             by_row = src.rearrange("g (q r) n -> r q g n", r=4)
-            words = plane[:].bitcast(I32).rearrange("p (g w) -> p g w", g=groups)
+            words = plane.bitcast(I32).rearrange("p (g w) -> p g w", g=groups)
             for r in range(4):
                 queue.dma_start(out=words[first_row + r : P : 32], in_=by_row[r].bitcast(I32))
 
         def load_v(e, pieces=1):
-            raw = stream.tile([P, PASSES, PACK, N], F32, name="v_raw", tag="weights", align_bytes=ALIGN)
+            raw = stream.tile([P, PASSES, PACK, N], F32, name="v_raw", tag="weights", align_bytes=PAGE)
             dst = raw[:].rearrange("p s j n -> p s (j n)")
             src = wv[e].rearrange("(s p j) n -> p s (j n)", s=PASSES, j=PACK)
             step = PASSES // pieces
@@ -77,30 +78,26 @@ def tile_moe_qkv_s_kernel(
 
         nc.sync.dma_start(offsets[:], offs)
         nc.sync.dma_start(
-            out=tok_words[:].rearrange("p (s t) -> p s t", s=PASSES),
+            out=tok_words[:, : PASSES * T].rearrange("p (s t) -> p s t", s=PASSES),
             in_=x_words.rearrange("s p t d -> p s (t d)").bitcast(I32),
         )
         load_v(0)
-        load_scale_rows(nc.sync, tok_scales, 0, x_scales)
+        load_scale_rows(nc.sync, tok_scales[:, : PASSES * T], 0, x_scales)
         nc.sync.dma_start(out=bias_rows[BIAS_ROW : BIAS_ROW + TILES, :], in_=bias.rearrange("(t p) e -> t (p e)", p=P))
-        load_scale_rows(nc.gpsimd, k_scales, WK_ROW, wk_scales.rearrange("e s b n -> (e s) b n"))
-        load_scale_rows(nc.gpsimd, q_scales, 0, wq_scales.rearrange("e s b n -> (e s) b n"))
+        load_scale_rows(nc.gpsimd, k_scales[:], WK_ROW, wk_scales.rearrange("e s b n -> (e s) b n"))
+        load_scale_rows(nc.gpsimd, q_scales[:], 0, wq_scales.rearrange("e s b n -> (e s) b n"))
         for e in range(1, SCALAR_V):
             load_v(e)
 
         slot_words, slot_scales = {}, {}
-        for g in range(E // GROUP):
-            listed = offsets[:, g * GROUP_SLOTS // 16 : (g + 1) * GROUP_SLOTS // 16]
-            for s in range(PASSES):
-                slot_words[g, s] = held.tile([P, GROUP_SLOTS], U32, name=f"slot_words{g}_{s}", align_bytes=ALIGN)
-                window = tok_words[:, s * T : (s + 1) * T].bitcast(U32)
-                nc.vector.tensor_copy(slot_words[g, s][:], window.indirect(listed))
-        for g in range(E // GROUP):
-            listed = offsets[:, g * GROUP_SLOTS // 16 : (g + 1) * GROUP_SLOTS // 16]
-            for s in range(PASSES):
-                slot_scales[g, s] = held.tile([P, GROUP_SLOTS], U8, name=f"slot_scales{g}_{s}", align_bytes=ALIGN)
-                window = tok_scales[:, s * T : (s + 1) * T]
-                nc.vector.tensor_copy(slot_scales[g, s][:], window.indirect(listed))
+        for s in range(PASSES):
+            slot_words[s] = held.tile([P, SLOTS], U32, name=f"slot_words{s}", align_bytes=64)
+            window = tok_words[:, s * T : (s + 2) * T].bitcast(U32)
+            nc.vector.tensor_copy(slot_words[s][:], window.indirect(offsets[:]))
+        for s in range(PASSES):
+            slot_scales[s] = held.tile([P, SLOTS], U8, name=f"slot_scales{s}", align_bytes=64)
+            window = tok_scales[:, s * T : (s + 2) * T]
+            nc.vector.tensor_copy(slot_scales[s][:], window.indirect(offsets[:]))
 
         def turn_bias():
             make_identity(nc, identity[:])
@@ -113,14 +110,13 @@ def tile_moe_qkv_s_kernel(
                 nc.vector.tensor_copy(out=bias_sb[:, first : first + count, :], in_=turned[:, :, BIAS_ROW : BIAS_ROW + TILES])
 
         def multiply(acc, e, s, codes, scales):
-            g, u = divmod(e, GROUP)
-            cols = slice(u * C, (u + 1) * C)
+            cols = slice(e * C, (e + 1) * C)
             nc.tensor.matmul_mx(
                 out=acc,
                 lhsT=codes,
                 lhsT_scale=scales,
-                rhs=slot_words[g, s][:, cols].bitcast(FP8X4),
-                rhs_scale=slot_scales[g, s][:, cols],
+                rhs=slot_words[s][:, cols].bitcast(FP8X4),
+                rhs_scale=slot_scales[s][:, cols],
                 start=(s == 0),
                 stop=(s == PASSES - 1),
             )
@@ -181,10 +177,10 @@ def tile_moe_qkv_s_kernel(
             first = (e * PASSES + s) * N + h * P
             return slice(first, first + P)
 
-        q_out = held.tile([P, HALVES, SLOTS], F32, name="q_out", align_bytes=ALIGN)
-        k_out = held.tile([P, HALVES, SLOTS], F32, name="k_out", align_bytes=ALIGN)
-        v_early = held.tile([P, HALVES, EARLY_V * C], F32, name="v_early", align_bytes=ALIGN)
-        v_late = held.tile([P, HALVES, C], F32, name="v_late", align_bytes=ALIGN)
+        q_out = held.tile([P, HALVES, SLOTS], F32, name="q_out", align_bytes=PAGE)
+        k_out = held.tile([P, HALVES, SLOTS], F32, name="k_out", align_bytes=PAGE)
+        v_early = held.tile([P, HALVES, EARLY_V * C], F32, name="v_early", align_bytes=PAGE)
+        v_late = held.tile([P, HALVES, C], F32, name="v_late", align_bytes=PAGE)
 
         def project_q(e):
             project(
@@ -213,7 +209,7 @@ def tile_moe_qkv_s_kernel(
         last = E - 1
 
         round_v(0)
-        k_codes = stream.tile([P, E * PASSES, N], I32, name="k_codes", tag="weights", align_bytes=ALIGN)
+        k_codes = stream.tile([P, E * PASSES, N], I32, name="k_codes", tag="weights", align_bytes=PAGE)
         nc.sync.dma_start(
             out=k_codes[:],
             in_=wk_words.rearrange("e s p n d -> p (e s) (n d)").bitcast(I32),
@@ -221,7 +217,7 @@ def tile_moe_qkv_s_kernel(
         round_v(1)
         load_v(4)
         round_v(2)
-        q_codes = stream.tile([P, E * PASSES, 2 * N], U8, name="q_codes", tag="weights", align_bytes=ALIGN)
+        q_codes = stream.tile([P, E * PASSES, 2 * N], U8, name="q_codes", tag="weights", align_bytes=PAGE)
         q_source = wq_words.rearrange("e s p b -> p (e s) b").bitcast(I32)
         for g in range(E // GROUP):
             part = slice(g * GROUP * PASSES, (g + 1) * GROUP * PASSES)

@@ -24,14 +24,13 @@ PACK = 4
 PASSES = K // (P * PACK)
 HALVES = N // P
 SLOTS = E * C
-GROUP = 3
 WK_ROW = 4
 TILES = 3 * HALVES
 PER_BANK = 4
-SCALAR_V = 4
+SCALAR_V = 3
 RING = 4
 BIAS_ROW = 16
-EARLY_V = E - 1
+EARLY_V = E - 2
 
 
 def tile_moe_qkv_s_kernel(
@@ -76,17 +75,17 @@ def tile_moe_qkv_s_kernel(
                 nc.sync.dma_start(out=dst[:, s : s + step], in_=src[:, s : s + step])
             v_raw[e] = [raw[:, s] for s in range(PASSES)]
 
-        nc.sync.dma_start(offsets[:], offs)
         nc.sync.dma_start(
             out=tok_words[:, : PASSES * T].rearrange("p (s t) -> p s t", s=PASSES),
             in_=x_words.rearrange("s p t d -> p s (t d)").bitcast(I32),
         )
+        nc.sync.dma_start(offsets[:], offs)
         load_v(0)
         load_scale_rows(nc.sync, tok_scales[:, : PASSES * T], 0, x_scales)
         nc.sync.dma_start(out=bias_rows[BIAS_ROW : BIAS_ROW + TILES, :], in_=bias.rearrange("(t p) e -> t (p e)", p=P))
         load_scale_rows(nc.gpsimd, k_scales[:], WK_ROW, wk_scales.rearrange("e s b n -> (e s) b n"))
         load_scale_rows(nc.gpsimd, q_scales[:], 0, wq_scales.rearrange("e s b n -> (e s) b n"))
-        for e in range(1, SCALAR_V):
+        for e in range(1, RING):
             load_v(e)
 
         slot_words, slot_scales = {}, {}
@@ -121,8 +120,8 @@ def tile_moe_qkv_s_kernel(
                 stop=(s == PASSES - 1),
             )
 
-        def project(e, proj, codes, scales, staged, on_vector):
-            result = staged[:, :, e * C : (e + 1) * C]
+        def project(e, proj, codes, scales, staged, on_vector, first=0):
+            result = staged[:, :, (e - first) * C : (e - first + 1) * C]
             acc = psum.tile([P, HALVES, C], F32, name="acc")
             for h in range(HALVES):
                 for s in range(PASSES):
@@ -146,7 +145,12 @@ def tile_moe_qkv_s_kernel(
 
         def round_piece(key, raw, on_vector):
             width = raw.shape[2]
-            tile = held.tile([P, width, PACK], BF16, name="v_grouped%d_%d_%d" % key, align_bytes=ALIGN)
+            e, s, h = key
+            shared = {1: 1, SCALAR_V: 1}.get(e, e)
+            tile = held.tile(
+                [P, width, PACK], BF16, name="v_grouped%d_%d_%d" % key,
+                tag="v_grouped%d_%d_%d" % (shared, s, h), align_bytes=ALIGN,
+            )
             src = raw.rearrange("p j (c i) -> p c j i", i=4)
             dst = tile[:].rearrange("p (c i) j -> p c j i", i=4)
             if on_vector:
@@ -180,7 +184,7 @@ def tile_moe_qkv_s_kernel(
         q_out = held.tile([P, HALVES, SLOTS], F32, name="q_out", align_bytes=PAGE)
         k_out = held.tile([P, HALVES, SLOTS], F32, name="k_out", align_bytes=PAGE)
         v_early = held.tile([P, HALVES, EARLY_V * C], F32, name="v_early", align_bytes=PAGE)
-        v_late = held.tile([P, HALVES, C], F32, name="v_late", align_bytes=PAGE)
+        v_late = held.tile([P, HALVES, (E - EARLY_V) * C], F32, name="v_late", align_bytes=PAGE)
 
         def project_q(e):
             project(
@@ -203,7 +207,7 @@ def tile_moe_qkv_s_kernel(
                 e, 2,
                 lambda s, h: v_codes[e, s, 0][:, h * P : (h + 1) * P].bitcast(FP8X4),
                 lambda s, h: v_scales[e, s, 0][:, h * P : (h + 1) * P],
-                v_early, on_vector=True,
+                v_early if e < EARLY_V else v_late, on_vector=True, first=0 if e < EARLY_V else EARLY_V,
             )
 
         last = E - 1
@@ -219,24 +223,25 @@ def tile_moe_qkv_s_kernel(
         round_v(2)
         q_codes = stream.tile([P, E * PASSES, 2 * N], U8, name="q_codes", tag="weights", align_bytes=PAGE)
         q_source = wq_words.rearrange("e s p b -> p (e s) b").bitcast(I32)
-        for g in range(E // GROUP):
-            part = slice(g * GROUP * PASSES, (g + 1) * GROUP * PASSES)
-            nc.sync.dma_start(out=q_codes[:].bitcast(I32)[:, part, :], in_=q_source[:, part, :])
+        nc.sync.dma_start(out=q_codes[:].bitcast(I32), in_=q_source)
+        turn_bias()
+        quantize_v(0)
+        quantize_v(1)
+        project_v(0)
         round_v(3)
         load_v(last, pieces=PASSES)
-        turn_bias()
-        for e in range(SCALAR_V):
-            quantize_v(e)
-            if e > 0:
-                project_v(e - 1)
+        project_v(1)
+        quantize_v(2)
+        quantize_v(3)
+        project_v(2)
         round_v(4)
         project_v(3)
+        store(2, 0, v_early)
         for e in range(E):
             project_k(e)
         store(1, 0, k_out)
         quantize_v(4)
         project_v(4)
-        store(2, 0, v_early)
         for e in range(3):
             project_q(e)
         round_piece((last, 0, 0), v_raw[last][0], on_vector=True)
@@ -256,7 +261,7 @@ def tile_moe_qkv_s_kernel(
             multiply(accs[h][:], last, 1, v_codes[last, 1, h][:].bitcast(FP8X4), v_scales[last, 1, h][:])
         columns = bias_sb[:, last, 2 * HALVES : 3 * HALVES]
         nc.vector.tensor_scalar(
-            out=v_late[:, 0, :], in0=accs[0][:], scalar1=columns[:, 0:1], scalar2=None, op0=ADD
+            out=v_late[:, 0, C:], in0=accs[0][:], scalar1=columns[:, 0:1], scalar2=None, op0=ADD
         )
-        nc.scalar.activation(out=v_late[:, 1, :], in_=accs[1][:], func=IDENTITY, bias=columns[:, 1:2])
+        nc.scalar.activation(out=v_late[:, 1, C:], in_=accs[1][:], func=IDENTITY, bias=columns[:, 1:2])
         store(2, EARLY_V * C, v_late)

@@ -30,7 +30,8 @@ PER_BANK = 4
 SCALAR_V = 3
 RING = 4
 BIAS_ROW = 16
-EARLY_V = E - 2
+EARLY = E - 2
+K_FIRST = 2
 
 
 def tile_moe_qkv_s_kernel(
@@ -50,13 +51,14 @@ def tile_moe_qkv_s_kernel(
         k_scales = held.tile([P, E * PASSES * N], U8, name="k_scales", align_bytes=ALIGN)
         bias_rows = held.tile([P, P * E], F32, name="bias_rows", align_bytes=ALIGN)
         bias_sb = held.tile([P, E, TILES], F32, name="bias_sb")
+        bias_q = held.tile([P, E, HALVES], F32, name="bias_q", tag="after_q", align_bytes=ALIGN)
         identity = held.tile([P, P], F32, name="identity")
         v_raw = {}
 
         nc.gpsimd.memset(bias_rows[:], 0.0)
         nc.vector.memset(tok_scales[:].bitcast(I32), 0)
-        nc.vector.memset(k_scales[:].bitcast(I32), 0)
         nc.vector.memset(q_scales[:].bitcast(I32), 0)
+        nc.vector.memset(k_scales[:].bitcast(I32), 0)
         nc.vector.memset(tok_words[:, PASSES * T :], 0)
 
         def load_scale_rows(queue, plane, first_row, src):
@@ -83,8 +85,8 @@ def tile_moe_qkv_s_kernel(
         load_v(0)
         load_scale_rows(nc.sync, tok_scales[:, : PASSES * T], 0, x_scales)
         nc.sync.dma_start(out=bias_rows[BIAS_ROW : BIAS_ROW + TILES, :], in_=bias.rearrange("(t p) e -> t (p e)", p=P))
-        load_scale_rows(nc.gpsimd, k_scales[:], WK_ROW, wk_scales.rearrange("e s b n -> (e s) b n"))
         load_scale_rows(nc.gpsimd, q_scales[:], 0, wq_scales.rearrange("e s b n -> (e s) b n"))
+        load_scale_rows(nc.gpsimd, k_scales[:], WK_ROW, wk_scales.rearrange("e s b n -> (e s) b n"))
         for e in range(1, RING):
             load_v(e)
 
@@ -107,6 +109,9 @@ def tile_moe_qkv_s_kernel(
                 for i in range(count):
                     nc.tensor.transpose(turned[:, i, :], by_expert[:, first + i, :], identity[:])
                 nc.vector.tensor_copy(out=bias_sb[:, first : first + count, :], in_=turned[:, :, BIAS_ROW : BIAS_ROW + TILES])
+                nc.vector.tensor_copy(
+                    out=bias_q[:, first : first + count, :], in_=turned[:, :, BIAS_ROW : BIAS_ROW + HALVES]
+                )
 
         def multiply(acc, e, s, codes, scales):
             cols = slice(e * C, (e + 1) * C)
@@ -126,7 +131,7 @@ def tile_moe_qkv_s_kernel(
             for h in range(HALVES):
                 for s in range(PASSES):
                     multiply(acc[:, h, :], e, s, codes(s, h), scales(s, h))
-            columns = bias_sb[:, e, proj * HALVES : (proj + 1) * HALVES]
+            columns = bias_q[:, e, :] if proj == 0 else bias_sb[:, e, proj * HALVES : (proj + 1) * HALVES]
             if on_vector:
                 spread = columns.unsqueeze(2).to_broadcast([P, HALVES, C])
                 nc.vector.tensor_tensor(out=result, in0=acc[:], in1=spread, op=ADD)
@@ -143,14 +148,10 @@ def tile_moe_qkv_s_kernel(
 
         v_grouped, v_codes, v_scales = {}, {}, {}
 
-        def round_piece(key, raw, on_vector):
-            width = raw.shape[2]
-            e, s, h = key
-            shared = {1: 1, SCALAR_V: 1}.get(e, e)
-            tile = held.tile(
-                [P, width, PACK], BF16, name="v_grouped%d_%d_%d" % key,
-                tag="v_grouped%d_%d_%d" % (shared, s, h), align_bytes=ALIGN,
-            )
+        def grouped(name, width, tag):
+            return held.tile([P, width, PACK], BF16, name=name, tag=tag, align_bytes=PAGE if tag.startswith("gate_k") else ALIGN)
+
+        def round_piece(key, raw, on_vector, tile):
             src = raw.rearrange("p j (c i) -> p c j i", i=4)
             dst = tile[:].rearrange("p (c i) j -> p c j i", i=4)
             if on_vector:
@@ -169,9 +170,12 @@ def tile_moe_qkv_s_kernel(
                 in_=v_grouped[key][:].rearrange("p n j -> p (n j)"),
             )
 
-        def round_v(e):
+        def round_v(e, tiles):
             for s in range(PASSES):
-                round_piece((e, s, 0), v_raw[e][s], on_vector=(e >= SCALAR_V))
+                round_piece((e, s, 0), v_raw[e][s], e >= SCALAR_V, tiles[s])
+
+        def own(e):
+            return [grouped(f"grouped{e}_{s}", N, f"grouped{e}_{s}") for s in range(PASSES)]
 
         def quantize_v(e):
             for s in range(PASSES):
@@ -182,24 +186,25 @@ def tile_moe_qkv_s_kernel(
             return slice(first, first + P)
 
         q_out = held.tile([P, HALVES, SLOTS], F32, name="q_out", align_bytes=PAGE)
-        k_out = held.tile([P, HALVES, SLOTS], F32, name="k_out", align_bytes=PAGE)
-        v_early = held.tile([P, HALVES, EARLY_V * C], F32, name="v_early", align_bytes=PAGE)
-        v_late = held.tile([P, HALVES, (E - EARLY_V) * C], F32, name="v_late", align_bytes=PAGE)
+        v_out = held.tile([P, HALVES, SLOTS], F32, name="v_out", align_bytes=PAGE)
+        k_early = held.tile([P, HALVES, EARLY * C], F32, name="k_early", align_bytes=PAGE)
+        k_late = held.tile([P, HALVES, (E - EARLY) * C], F32, name="k_late", align_bytes=PAGE)
 
         def project_q(e):
             project(
                 e, 0,
                 lambda s, h: q_codes[:, e * PASSES + s, h * 2 * P : (h + 1) * 2 * P].bitcast(FP4X4),
                 lambda s, h: q_scales[:, plane_cols(e, s, h)],
-                q_out, on_vector=(e % 2 == 0),
+                q_out, on_vector=False,
             )
 
         def project_k(e):
+            first = 0 if e < EARLY else EARLY
             project(
                 e, 1,
-                lambda s, h: k_codes[:, e * PASSES + s, h * P : (h + 1) * P].bitcast(FP8X4),
+                lambda s, h: k_codes[e][:, s, h * P : (h + 1) * P].bitcast(FP8X4),
                 lambda s, h: k_scales[WK_ROW:P, plane_cols(e, s, h)],
-                k_out, on_vector=False,
+                k_early if e < EARLY else k_late, on_vector=(e % 2 == 1), first=first,
             )
 
         def project_v(e):
@@ -207,61 +212,59 @@ def tile_moe_qkv_s_kernel(
                 e, 2,
                 lambda s, h: v_codes[e, s, 0][:, h * P : (h + 1) * P].bitcast(FP8X4),
                 lambda s, h: v_scales[e, s, 0][:, h * P : (h + 1) * P],
-                v_early if e < EARLY_V else v_late, on_vector=True, first=0 if e < EARLY_V else EARLY_V,
+                v_out, on_vector=(e != 4),
             )
 
         last = E - 1
 
-        round_v(0)
-        k_codes = stream.tile([P, E * PASSES, N], I32, name="k_codes", tag="weights", align_bytes=PAGE)
-        nc.sync.dma_start(
-            out=k_codes[:],
-            in_=wk_words.rearrange("e s p n d -> p (e s) (n d)").bitcast(I32),
-        )
-        round_v(1)
-        load_v(4)
-        round_v(2)
+        round_v(0, own(0))
         q_codes = stream.tile([P, E * PASSES, 2 * N], U8, name="q_codes", tag="weights", align_bytes=PAGE)
         q_source = wq_words.rearrange("e s p b -> p (e s) b").bitcast(I32)
         nc.sync.dma_start(out=q_codes[:].bitcast(I32), in_=q_source)
+        round_v(1, [grouped(f"grouped1_{s}", N, f"gate_k{s}") for s in range(PASSES)])
+        load_v(4)
+        round_v(2, own(2))
+        load_v(last, pieces=PASSES)
         turn_bias()
         quantize_v(0)
         quantize_v(1)
         project_v(0)
-        round_v(3)
-        load_v(last, pieces=PASSES)
+        round_v(3, [grouped(f"grouped3_{s}", N, f"gate_k{s}") for s in range(PASSES)])
         project_v(1)
-        quantize_v(2)
-        quantize_v(3)
-        project_v(2)
-        round_v(4)
-        project_v(3)
-        store(2, 0, v_early)
-        for e in range(E):
-            project_k(e)
-        store(1, 0, k_out)
-        quantize_v(4)
-        project_v(4)
         for e in range(3):
             project_q(e)
-        round_piece((last, 0, 0), v_raw[last][0], on_vector=True)
+        quantize_v(2)
+        quantize_v(3)
+        k_source = wk_words.rearrange("e s p n d -> p (e s) (n d)").bitcast(I32)
+        k_codes = {}
+        for i, experts in enumerate((range(K_FIRST), range(K_FIRST, E))):
+            piece = held.tile(
+                [P, len(experts) * PASSES, N], I32, name=f"k_codes{i}", tag=f"gate_k{i}", align_bytes=PAGE
+            )
+            nc.sync.dma_start(out=piece[:], in_=k_source[:, experts.start * PASSES : experts.stop * PASSES])
+            for e in experts:
+                k_codes[e] = piece[:, (e - experts.start) * PASSES : (e - experts.start + 1) * PASSES]
+        project_v(2)
         project_q(3)
-        quantize_piece((last, 0, 0))
+        project_v(3)
         project_q(4)
         project_q(5)
         store(0, 0, q_out)
-        accs = [psum.tile([P, C], F32, name="acc") for h in range(HALVES)]
-        for h in range(HALVES):
-            cols = slice(h * P, (h + 1) * P)
-            multiply(accs[h][:], last, 0, v_codes[last, 0, 0][:, cols].bitcast(FP8X4), v_scales[last, 0, 0][:, cols])
-        for h in range(HALVES):
-            round_piece((last, 1, h), v_raw[last][1][:, :, h * P : (h + 1) * P], on_vector=(h == 0))
-        for h in range(HALVES):
-            quantize_piece((last, 1, h))
-            multiply(accs[h][:], last, 1, v_codes[last, 1, h][:].bitcast(FP8X4), v_scales[last, 1, h][:])
-        columns = bias_sb[:, last, 2 * HALVES : 3 * HALVES]
-        nc.vector.tensor_scalar(
-            out=v_late[:, 0, C:], in0=accs[0][:], scalar1=columns[:, 0:1], scalar2=None, op0=ADD
-        )
-        nc.scalar.activation(out=v_late[:, 1, C:], in_=accs[1][:], func=IDENTITY, bias=columns[:, 1:2])
-        store(2, EARLY_V * C, v_late)
+        late = grouped("grouped_late", 3 * N, "grouped2_1")
+        final = grouped("grouped_final", N, "after_q")
+        round_v(4, [late[:, :N], late[:, N : 2 * N]])
+        round_piece((last, 0, 0), v_raw[last][0], False, final)
+        quantize_v(4)
+        round_piece((last, 1, 0), v_raw[last][1], True, late[:, 2 * N :])
+        project_v(4)
+        quantize_piece((last, 0, 0))
+        quantize_piece((last, 1, 0))
+        for e in range(K_FIRST):
+            project_k(e)
+        project_v(last)
+        store(2, 0, v_out)
+        for e in range(K_FIRST, E):
+            project_k(e)
+            if e == EARLY - 1:
+                store(1, 0, k_early)
+        store(1, EARLY * C, k_late)

@@ -24,7 +24,7 @@ PACK = 4
 PASSES = K // (P * PACK)
 HALVES = N // P
 SLOTS = E * C
-WK_ROW = 4
+WK_ROW = 8
 TILES = 3 * HALVES
 PER_BANK = 4
 SCALAR_V = 3
@@ -84,10 +84,11 @@ def tile_moe_qkv_s_kernel(
         nc.sync.dma_start(offsets[:], offs)
         load_v(0)
         load_scale_rows(nc.sync, tok_scales[:, : PASSES * T], 0, x_scales)
-        nc.sync.dma_start(out=bias_rows[BIAS_ROW : BIAS_ROW + TILES, :], in_=bias.rearrange("(t p) e -> t (p e)", p=P))
         load_scale_rows(nc.gpsimd, q_scales[:], 0, wq_scales.rearrange("e s b n -> (e s) b n"))
         load_scale_rows(nc.gpsimd, k_scales[:], WK_ROW, wk_scales.rearrange("e s b n -> (e s) b n"))
-        for e in range(1, RING):
+        load_v(1)
+        nc.sync.dma_start(out=bias_rows[BIAS_ROW : BIAS_ROW + TILES, :], in_=bias.rearrange("(t p) e -> t (p e)", p=P))
+        for e in range(2, RING):
             load_v(e)
 
         slot_words, slot_scales = {}, {}

@@ -238,10 +238,10 @@ def tile_moe_qkv_s_kernel(
         quantize_v(3)
         k_source = wk_words.rearrange("e s p n d -> p (e s) (n d)").bitcast(I32)
         k_codes = {}
-        for i, experts in enumerate((range(K_FIRST), range(K_FIRST, E))):
-            piece = held.tile(
-                [P, len(experts) * PASSES, N], I32, name=f"k_codes{i}", tag=f"gate_k{i}", align_bytes=PAGE
-            )
+        for i in range(E // K_FIRST):
+            experts = range(i * K_FIRST, (i + 1) * K_FIRST)
+            pool, tag = (stream, "weights") if i == 0 else (held, f"gate_k{i - 1}")
+            piece = pool.tile([P, len(experts) * PASSES, N], I32, name=f"k_codes{i}", tag=tag, align_bytes=PAGE)
             nc.sync.dma_start(out=piece[:], in_=k_source[:, experts.start * PASSES : experts.stop * PASSES])
             for e in experts:
                 k_codes[e] = piece[:, (e - experts.start) * PASSES : (e - experts.start + 1) * PASSES]

@@ -30,7 +30,6 @@ PER_BANK = 4
 SCALAR_V = 3
 RING = 4
 BIAS_ROW = 16
-EARLY = E - 2
 K_FIRST = 2
 
 
@@ -188,8 +187,7 @@ def tile_moe_qkv_s_kernel(
 
         q_out = held.tile([P, HALVES, SLOTS], F32, name="q_out", align_bytes=PAGE)
         v_out = held.tile([P, HALVES, SLOTS], F32, name="v_out", align_bytes=PAGE)
-        k_early = held.tile([P, HALVES, EARLY * C], F32, name="k_early", align_bytes=PAGE)
-        k_late = held.tile([P, HALVES, (E - EARLY) * C], F32, name="k_late", align_bytes=PAGE)
+        k_out = [held.tile([P, HALVES, K_FIRST * C], F32, name=f"k_out{i}", align_bytes=PAGE) for i in range(E // K_FIRST)]
 
         def project_q(e):
             project(
@@ -200,12 +198,12 @@ def tile_moe_qkv_s_kernel(
             )
 
         def project_k(e):
-            first = 0 if e < EARLY else EARLY
+            first = e - e % K_FIRST
             project(
                 e, 1,
                 lambda s, h: k_codes[e][:, s, h * P : (h + 1) * P].bitcast(FP8X4),
                 lambda s, h: k_scales[WK_ROW:P, plane_cols(e, s, h)],
-                k_early if e < EARLY else k_late, on_vector=(e % 2 == 1), first=first,
+                k_out[e // K_FIRST], on_vector=(e % 2 == 1), first=first,
             )
 
         def project_v(e):
@@ -262,10 +260,10 @@ def tile_moe_qkv_s_kernel(
         quantize_piece((last, 1, 0))
         for e in range(K_FIRST):
             project_k(e)
+        store(1, 0, k_out[0])
         project_v(last)
         store(2, 0, v_out)
         for e in range(K_FIRST, E):
             project_k(e)
-            if e == EARLY - 1:
-                store(1, 0, k_early)
-        store(1, EARLY * C, k_late)
+            if e % K_FIRST == K_FIRST - 1:
+                store(1, (e - e % K_FIRST) * C, k_out[e // K_FIRST])

@@ -49,7 +49,7 @@ def tile_moe_qkv_s_kernel(
         q_scales = held.tile([P, E * PASSES * N], U8, name="q_scales", align_bytes=ALIGN)
         k_scales = held.tile([P, E * PASSES * N], U8, name="k_scales", align_bytes=ALIGN)
         bias_rows = held.tile([P, P * E], F32, name="bias_rows", align_bytes=ALIGN)
-        bias_sb = held.tile([P, E, TILES], F32, name="bias_sb")
+        bias_sb = held.tile([P, E, TILES - HALVES], F32, name="bias_sb")
         bias_q = held.tile([P, E, HALVES], F32, name="bias_q", tag="after_q", align_bytes=ALIGN)
         identity = held.tile([P, P], F32, name="identity")
         v_raw = {}
@@ -108,7 +108,7 @@ def tile_moe_qkv_s_kernel(
                 turned = psum_bias.tile([P, count, P], F32, name=f"turned{first}")
                 for i in range(count):
                     nc.tensor.transpose(turned[:, i, :], by_expert[:, first + i, :], identity[:])
-                nc.vector.tensor_copy(out=bias_sb[:, first : first + count, :], in_=turned[:, :, BIAS_ROW : BIAS_ROW + TILES])
+                nc.vector.tensor_copy(out=bias_sb[:, first : first + count, :], in_=turned[:, :, BIAS_ROW + HALVES : BIAS_ROW + TILES])
                 nc.vector.tensor_copy(
                     out=bias_q[:, first : first + count, :], in_=turned[:, :, BIAS_ROW : BIAS_ROW + HALVES]
                 )
@@ -131,7 +131,7 @@ def tile_moe_qkv_s_kernel(
             for h in range(HALVES):
                 for s in range(PASSES):
                     multiply(acc[:, h, :], e, s, codes(s, h), scales(s, h))
-            columns = bias_q[:, e, :] if proj == 0 else bias_sb[:, e, proj * HALVES : (proj + 1) * HALVES]
+            columns = bias_q[:, e, :] if proj == 0 else bias_sb[:, e, (proj - 1) * HALVES : proj * HALVES]
             if on_vector:
                 spread = columns.unsqueeze(2).to_broadcast([P, HALVES, C])
                 nc.vector.tensor_tensor(out=result, in0=acc[:], in1=spread, op=ADD)

@@ -219,7 +219,8 @@ def tile_moe_qkv_s_kernel(
         round_v(0, own(0))
         q_codes = stream.tile([P, E * PASSES, 2 * N], U8, name="q_codes", tag="weights", align_bytes=PAGE)
         q_source = wq_words.rearrange("e s p b -> p (e s) b").bitcast(I32)
-        nc.sync.dma_start(out=q_codes[:].bitcast(I32), in_=q_source)
+        for g in range(0, E * PASSES, E):
+            nc.sync.dma_start(out=q_codes[:, g : g + E].bitcast(I32), in_=q_source[:, g : g + E])
         round_v(1, [grouped(f"grouped1_{s}", N, f"gate_k{s}") for s in range(PASSES)])
         load_v(4)
         round_v(2, own(2))

@@ -84,11 +84,12 @@ def tile_moe_qkv_s_kernel(
         load_v(0)
         load_scale_rows(nc.sync, tok_scales[:, : PASSES * T], 0, x_scales)
         load_scale_rows(nc.gpsimd, q_scales[:], 0, wq_scales.rearrange("e s b n -> (e s) b n"))
-        load_scale_rows(nc.gpsimd, k_scales[:], WK_ROW, wk_scales.rearrange("e s b n -> (e s) b n"))
         load_v(1)
         nc.sync.dma_start(out=bias_rows[BIAS_ROW : BIAS_ROW + TILES, :], in_=bias.rearrange("(t p) e -> t (p e)", p=P))
         for e in range(2, RING):
             load_v(e)
+
+        load_scale_rows(nc.sync, k_scales[:], WK_ROW, wk_scales.rearrange("e s b n -> (e s) b n"))
 
         slot_words, slot_scales = {}, {}
         for s in range(PASSES):

@@ -83,12 +83,11 @@ def tile_moe_qkv_s_kernel(
         nc.sync.dma_start(offsets[:], offs)
         load_v(0)
         load_scale_rows(nc.sync, tok_scales[:, : PASSES * T], 0, x_scales)
-        load_scale_rows(nc.gpsimd, q_scales[:], 0, wq_scales.rearrange("e s b n -> (e s) b n"))
         load_v(1)
         nc.sync.dma_start(out=bias_rows[BIAS_ROW : BIAS_ROW + TILES, :], in_=bias.rearrange("(t p) e -> t (p e)", p=P))
-        for e in range(2, RING):
-            load_v(e)
-
+        load_v(2)
+        load_scale_rows(nc.sync, q_scales[:], 0, wq_scales.rearrange("e s b n -> (e s) b n"))
+        load_v(3)
         load_scale_rows(nc.sync, k_scales[:], WK_ROW, wk_scales.rearrange("e s b n -> (e s) b n"))
 
         slot_words, slot_scales = {}, {}

from contextlib import ExitStack

import concourse.mybir as mybir
from concourse.masks import make_identity

K, T, E, C, N = 1024, 512, 6, 128, 256
FLOPS = 2 * K * 3 * N * E * C

F32 = mybir.dt.float32
BF16 = mybir.dt.bfloat16
I32 = mybir.dt.int32
U32 = mybir.dt.uint32
U16 = mybir.dt.uint16
U8 = mybir.dt.uint8
FP8X4 = mybir.dt.float8_e4m3fn_x4
FP4X4 = mybir.dt.float4_e2m1fn_x4
ADD = mybir.AluOpType.add
IDENTITY = mybir.ActivationFunctionType.Identity

P = 128
ALIGN = 256
PAGE = 4096
PACK = 4
PASSES = K // (P * PACK)
HALVES = N // P
SLOTS = E * C
WK_ROW = 8
TILES = 3 * HALVES
PER_BANK = 4
SCALAR_V = 3
RING = 4
BIAS_ROW = 16
K_FIRST = 2


def tile_moe_qkv_s_kernel(
    tc, x_words, x_scales, wq_words, wq_scales, wk_words, wk_scales, wv, bias, offs, out
):
    nc = tc.nc
    with ExitStack() as ctx:
        held = ctx.enter_context(tc.tile_pool(name="held", bufs=1))
        stream = ctx.enter_context(tc.tile_pool(name="stream", bufs=RING))
        psum = ctx.enter_context(tc.psum_pool(name="psum", bufs=6))
        psum_bias = ctx.enter_context(tc.psum_pool(name="psum_bias", bufs=1))

        offsets = held.tile([P, SLOTS // 16], U16, name="offsets", align_bytes=ALIGN)
        tok_words = held.tile([P, (PASSES + 1) * T], I32, name="tok_words", align_bytes=PAGE)
        tok_scales = held.tile([P, (PASSES + 1) * T], U8, name="tok_scales", align_bytes=ALIGN)
        q_scales = held.tile([P, E * PASSES * N], U8, name="q_scales", align_bytes=ALIGN)
        k_scales = held.tile([P, E * PASSES * N], U8, name="k_scales", align_bytes=ALIGN)
        bias_rows = held.tile([P, P * E], F32, name="bias_rows", align_bytes=ALIGN)
        bias_sb = held.tile([P, E, TILES - HALVES], F32, name="bias_sb")
        bias_q = held.tile([P, E, HALVES], F32, name="bias_q", tag="after_q", align_bytes=ALIGN)
        identity = held.tile([P, P], F32, name="identity")
        v_raw = {}

        nc.gpsimd.memset(bias_rows[:], 0.0)
        nc.vector.memset(tok_scales[:].bitcast(I32), 0)
        nc.vector.memset(q_scales[:].bitcast(I32), 0)
        nc.vector.memset(k_scales[:].bitcast(I32), 0)
        nc.vector.memset(tok_words[:, PASSES * T :], 0)

        def load_scale_rows(queue, plane, first_row, src):
            groups = src.shape[0]
            by_row = src.rearrange("g (q r) n -> r q g n", r=4)
            words = plane.bitcast(I32).rearrange("p (g w) -> p g w", g=groups)
            for r in range(4):
                queue.dma_start(out=words[first_row + r : P : 32], in_=by_row[r].bitcast(I32))

        def load_v(e, pieces=1):
            raw = stream.tile([P, PASSES, PACK, N], F32, name="v_raw", tag="weights", align_bytes=PAGE)
            dst = raw[:].rearrange("p s j n -> p s (j n)")
            src = wv[e].rearrange("(s p j) n -> p s (j n)", s=PASSES, j=PACK)
            step = PASSES // pieces
            for s in range(0, PASSES, step):
                nc.sync.dma_start(out=dst[:, s : s + step], in_=src[:, s : s + step])
            v_raw[e] = [raw[:, s] for s in range(PASSES)]

        nc.sync.dma_start(
            out=tok_words[:, : PASSES * T].rearrange("p (s t) -> p s t", s=PASSES),
            in_=x_words.rearrange("s p t d -> p s (t d)").bitcast(I32),
        )
        nc.sync.dma_start(offsets[:], offs)
        load_v(0)
        load_scale_rows(nc.sync, tok_scales[:, : PASSES * T], 0, x_scales)
        load_v(1)
        nc.sync.dma_start(out=bias_rows[BIAS_ROW : BIAS_ROW + TILES, :], in_=bias.rearrange("(t p) e -> t (p e)", p=P))
        load_v(2)
        load_scale_rows(nc.sync, q_scales[:], 0, wq_scales.rearrange("e s b n -> (e s) b n"))
        load_v(3)
        load_scale_rows(nc.sync, k_scales[:], WK_ROW, wk_scales.rearrange("e s b n -> (e s) b n"))

        slot_words, slot_scales = {}, {}
        for s in range(PASSES):
            slot_words[s] = held.tile([P, SLOTS], U32, name=f"slot_words{s}", align_bytes=64)
            window = tok_words[:, s * T : (s + 2) * T].bitcast(U32)
            nc.vector.tensor_copy(slot_words[s][:], window.indirect(offsets[:]))
        for s in range(PASSES):
            slot_scales[s] = held.tile([P, SLOTS], U8, name=f"slot_scales{s}", align_bytes=64)
            window = tok_scales[:, s * T : (s + 2) * T]
            nc.vector.tensor_copy(slot_scales[s][:], window.indirect(offsets[:]))

        def turn_bias():
            make_identity(nc, identity[:])
            by_expert = bias_rows[:].rearrange("t (p e) -> t e p", e=E)
            for first in range(0, E, PER_BANK):
                count = min(PER_BANK, E - first)
                turned = psum_bias.tile([P, count, P], F32, name=f"turned{first}")
                for i in range(count):
                    nc.tensor.transpose(turned[:, i, :], by_expert[:, first + i, :], identity[:])
                nc.vector.tensor_copy(out=bias_sb[:, first : first + count, :], in_=turned[:, :, BIAS_ROW + HALVES : BIAS_ROW + TILES])
                nc.vector.tensor_copy(
                    out=bias_q[:, first : first + count, :], in_=turned[:, :, BIAS_ROW : BIAS_ROW + HALVES]
                )

        def multiply(acc, e, s, codes, scales):
            cols = slice(e * C, (e + 1) * C)
            nc.tensor.matmul_mx(
                out=acc,
                lhsT=codes,
                lhsT_scale=scales,
                rhs=slot_words[s][:, cols].bitcast(FP8X4),
                rhs_scale=slot_scales[s][:, cols],
                start=(s == 0),
                stop=(s == PASSES - 1),
            )

        def project(e, proj, codes, scales, staged, on_vector, first=0):
            result = staged[:, :, (e - first) * C : (e - first + 1) * C]
            acc = psum.tile([P, HALVES, C], F32, name="acc")
            for h in range(HALVES):
                for s in range(PASSES):
                    multiply(acc[:, h, :], e, s, codes(s, h), scales(s, h))
            columns = bias_q[:, e, :] if proj == 0 else bias_sb[:, e, (proj - 1) * HALVES : proj * HALVES]
            if on_vector:
                spread = columns.unsqueeze(2).to_broadcast([P, HALVES, C])
                nc.vector.tensor_tensor(out=result, in0=acc[:], in1=spread, op=ADD)
            else:
                for h in range(HALVES):
                    nc.scalar.activation(
                        out=result[:, h, :], in_=acc[:, h, :], func=IDENTITY, bias=columns[:, h : h + 1]
                    )

        def store(proj, first, staged):
            width = staged.shape[2]
            rows = out[proj * N : (proj + 1) * N, first : first + width]
            nc.sync.dma_start(out=rows.rearrange("(h p) j -> p h j", p=P), in_=staged[:])

        v_grouped, v_codes, v_scales = {}, {}, {}

        def grouped(name, width, tag):
            return held.tile([P, width, PACK], BF16, name=name, tag=tag, align_bytes=PAGE if tag.startswith("gate_k") else ALIGN)

        def round_piece(key, raw, on_vector, tile):
            src = raw.rearrange("p j (c i) -> p c j i", i=4)
            dst = tile[:].rearrange("p (c i) j -> p c j i", i=4)
            if on_vector:
                nc.vector.tensor_copy(out=dst, in_=src)
            else:
                nc.scalar.copy(out=dst, in_=src)
            v_grouped[key] = tile

        def quantize_piece(key):
            width = v_grouped[key].shape[1]
            v_codes[key] = held.tile([P, width], U32, name="v_codes%d_%d_%d" % key, align_bytes=ALIGN)
            v_scales[key] = held.tile([P, width], U8, name="v_scales%d_%d_%d" % key, align_bytes=ALIGN)
            nc.vector.quantize_mx(
                out=v_codes[key][:].bitcast(FP8X4),
                scales=v_scales[key][:],
                in_=v_grouped[key][:].rearrange("p n j -> p (n j)"),
            )

        def round_v(e, tiles):
            for s in range(PASSES):
                round_piece((e, s, 0), v_raw[e][s], e >= SCALAR_V, tiles[s])

        def own(e):
            return [grouped(f"grouped{e}_{s}", N, f"grouped{e}_{s}") for s in range(PASSES)]

        def quantize_v(e):
            for s in range(PASSES):
                quantize_piece((e, s, 0))

        def plane_cols(e, s, h):
            first = (e * PASSES + s) * N + h * P
            return slice(first, first + P)

        q_out = held.tile([P, HALVES, SLOTS], F32, name="q_out", align_bytes=PAGE)
        v_out = held.tile([P, HALVES, SLOTS], F32, name="v_out", align_bytes=PAGE)
        k_out = [held.tile([P, HALVES, K_FIRST * C], F32, name=f"k_out{i}", align_bytes=PAGE) for i in range(E // K_FIRST)]

        def project_q(e):
            project(
                e, 0,
                lambda s, h: q_codes[:, e * PASSES + s, h * 2 * P : (h + 1) * 2 * P].bitcast(FP4X4),
                lambda s, h: q_scales[:, plane_cols(e, s, h)],
                q_out, on_vector=False,
            )

        def project_k(e):
            first = e - e % K_FIRST
            project(
                e, 1,
                lambda s, h: k_codes[e][:, s, h * P : (h + 1) * P].bitcast(FP8X4),
                lambda s, h: k_scales[WK_ROW:P, plane_cols(e, s, h)],
                k_out[e // K_FIRST], on_vector=(e % 2 == 1), first=first,
            )

        def project_v(e):
            project(
                e, 2,
                lambda s, h: v_codes[e, s, 0][:, h * P : (h + 1) * P].bitcast(FP8X4),
                lambda s, h: v_scales[e, s, 0][:, h * P : (h + 1) * P],
                v_out, on_vector=(e != 4),
            )

        last = E - 1

        round_v(0, own(0))
        q_codes = stream.tile([P, E * PASSES, 2 * N], U8, name="q_codes", tag="weights", align_bytes=PAGE)
        q_source = wq_words.rearrange("e s p b -> p (e s) b").bitcast(I32)
        for g in range(0, E * PASSES, E):
            nc.sync.dma_start(out=q_codes[:, g : g + E].bitcast(I32), in_=q_source[:, g : g + E])
        round_v(1, [grouped(f"grouped1_{s}", N, f"gate_k{s}") for s in range(PASSES)])
        load_v(4)
        round_v(2, own(2))
        load_v(last, pieces=PASSES)
        turn_bias()
        quantize_v(0)
        quantize_v(1)
        project_v(0)
        round_v(3, [grouped(f"grouped3_{s}", N, f"gate_k{s}") for s in range(PASSES)])
        project_v(1)
        for e in range(3):
            project_q(e)
        quantize_v(2)
        quantize_v(3)
        k_source = wk_words.rearrange("e s p n d -> p (e s) (n d)").bitcast(I32)
        k_codes = {}
        for i in range(E // K_FIRST):
            experts = range(i * K_FIRST, (i + 1) * K_FIRST)
            pool, tag = (stream, "weights") if i == 0 else (held, f"gate_k{i - 1}")
            piece = pool.tile([P, len(experts) * PASSES, N], I32, name=f"k_codes{i}", tag=tag, align_bytes=PAGE)
            nc.sync.dma_start(out=piece[:], in_=k_source[:, experts.start * PASSES : experts.stop * PASSES])
            for e in experts:
                k_codes[e] = piece[:, (e - experts.start) * PASSES : (e - experts.start + 1) * PASSES]
        project_v(2)
        project_q(3)
        project_v(3)
        project_q(4)
        project_q(5)
        store(0, 0, q_out)
        late = grouped("grouped_late", 3 * N, "grouped2_1")
        final = grouped("grouped_final", N, "after_q")
        round_v(4, [late[:, :N], late[:, N : 2 * N]])
        round_piece((last, 0, 0), v_raw[last][0], False, final)
        quantize_v(4)
        round_piece((last, 1, 0), v_raw[last][1], True, late[:, 2 * N :])
        project_v(4)
        quantize_piece((last, 0, 0))
        quantize_piece((last, 1, 0))
        for e in range(K_FIRST):
            project_k(e)
        store(1, 0, k_out[0])
        project_v(last)
        store(2, 0, v_out)
        for e in range(K_FIRST, E):
            project_k(e)
            if e % K_FIRST == K_FIRST - 1:
                store(1, (e - e % K_FIRST) * C, k_out[e // K_FIRST])
